import numpy as np
import ml_dtypes


def mxq(x, axis, fmt="e4m3"):
    dtype, down = {"e4m3": (ml_dtypes.float8_e4m3fn, 7), "e5m2": (ml_dtypes.float8_e5m2, 14)}[fmt]
    v = np.moveaxis(np.asarray(x, np.float32).astype(ml_dtypes.bfloat16).astype(np.float64), axis, -1)
    blocks = v.reshape(v.shape[:-1] + (-1, 32))
    amax = np.abs(blocks).max(-1, keepdims=True)
    byte = np.maximum(np.where(amax > 0, np.frexp(amax)[1] - 1 + 127, 0) - down, 1)
    scale = np.exp2(byte - 127.0)
    codes = (blocks / scale).astype(np.float32).astype(dtype).astype(np.float64)
    return np.moveaxis((codes * scale).reshape(v.shape), -1, axis)


WIDE = False


def mx_kscale(k):
    if not WIDE:
        return np.ones(k)
    levels = np.array([10, -10, 5, -5, 0])
    if k % 512:
        return np.exp2(np.random.permutation(np.resize(levels, k // 32))).repeat(32)
    a = np.empty((k // 512, 16))
    for p in range(k // 512):
        a[p, :8] = np.random.permutation(np.resize(levels, 8))
        for g in range(8):
            far = levels[np.abs(levels - a[p, g]) >= 10]
            a[p, g + 8] = far[np.random.randint(len(far))]
    return np.exp2(a.ravel()).repeat(32)


def f64(x):
    return np.asarray(x).astype(np.float64)


def striped(idx):
    return np.tile(idx.reshape(-1, 16).T, (8, 1)).astype(np.uint16)


def unstriped(offs):
    return offs[:16].T.reshape(-1).astype(np.int64)


def pack_weight(w):
    k, n = w.shape
    w = f64(np.asarray(w, np.float32).astype(ml_dtypes.bfloat16)).reshape(k // 32, 32, n)
    amax = np.abs(w).max(1)
    byte = np.clip(np.where(amax > 0, np.frexp(amax)[1] - 1 + 127 - 7, 1), 1, 254)
    scaled = (w * np.exp2(127.0 - byte)[:, None, :]).reshape(k, n).astype(np.float32)
    words = np.ascontiguousarray(scaled.reshape(k // 512, 128, 4, n).transpose(0, 1, 3, 2)).astype(ml_dtypes.float8_e4m3fn).view(np.uint8)
    return words, np.ascontiguousarray(byte.astype(np.uint8).reshape(k // 512, 16, n))


def unpack_weight(words, scales):
    g, p, n, _ = words.shape
    vals = np.ascontiguousarray(words).view(ml_dtypes.float8_e4m3fn).astype(np.float64) * np.repeat(np.exp2(scales.astype(np.float64) - 127.0), 8, axis=1)[..., None]
    return vals.transpose(0, 1, 3, 2).reshape(g * 512, n)


def sigmoid(v):
    return 1.0 / (1.0 + np.exp(-np.maximum(v, -700.0)))


K, T, N, U = 512, 1024, 256, 2048


def setup_inputs():
    n = np.random.standard_normal
    s = mx_kscale(K)[:, None]
    packed_xT = pack_weight(n((K, T)) * s)
    return {
        "x_words": packed_xT[0],
        "x_scales": packed_xT[1],
        "mem": n((N, U)).astype(np.float32),
        "w1": (n((K, N)) / np.sqrt(K) / s).astype(np.float32),
        "slot": striped(np.random.permutation(U)[:T]),
    }


def reference(x_words, x_scales, mem, w1, slot):
    xq = unpack_weight(x_words, x_scales)
    y = mxq(f64(w1), 0, "e4m3").T @ xq
    out = f64(mem).copy()
    out[:, unstriped(slot)] = f64(mem)[:, unstriped(slot)] * sigmoid(y)
    return out

@@ -1,0 +1,113 @@
+from contextlib import ExitStack
+
+import concourse.mybir as mybir
+
+K, T, N, U = 512, 1024, 256, 2048
+FLOPS = 2 * K * T * N
+
+F32 = mybir.dt.float32
+BF16 = mybir.dt.bfloat16
+I32 = mybir.dt.int32
+U32 = mybir.dt.uint32
+U16 = mybir.dt.uint16
+U8 = mybir.dt.uint8
+FP8X4 = mybir.dt.float8_e4m3fn_x4
+SIGMOID = mybir.ActivationFunctionType.Sigmoid
+MULT = mybir.AluOpType.mult
+
+P = 128
+PACK = 4
+HALF = 512
+LIST_ROWS = 16
+
+
+def tile_picked_widxput_gate_l_kernel(tc, x_words, x_scales, mem, w1, slot, out):
+    nc = tc.nc
+    with ExitStack() as ctx:
+        keep = ctx.enter_context(tc.tile_pool(name="keep", bufs=1))
+        psum = ctx.enter_context(tc.psum_pool(name="psum", bufs=1))
+
+        offsets = keep.tile([P, T // LIST_ROWS], U16, name="offsets")
+        x_plane = keep.tile([P, T], U8, name="x_plane", align_bytes=64)
+        x_codes = [keep.tile([P, HALF], U32, name="x_codes%d" % h, align_bytes=64) for h in range(2)]
+        w_raw = [keep.tile([P, PACK, P], F32, name="w_raw%d" % b, align_bytes=64) for b in range(2)]
+        w_grouped = [keep.tile([P, P, PACK], BF16, name="w_grouped%d" % b, align_bytes=64) for b in range(2)]
+        w_codes = [keep.tile([P, P], U32, name="w_codes%d" % b, align_bytes=64) for b in range(2)]
+        w_plane = [keep.tile([P, P], U8, name="w_plane%d" % b, align_bytes=64) for b in range(2)]
+        store = [keep.tile([P, U], F32, name="store%d" % b, align_bytes=64) for b in range(2)]
+        old = [keep.tile([P, T], F32, name="old%d" % b, align_bytes=64) for b in range(2)]
+        gate = [keep.tile([P, T], F32, name="gate%d" % b, align_bytes=64) for b in range(2)]
+        warm_in = keep.tile([P, 8], F32, name="warm_in")
+        warm_out = keep.tile([P, 8], F32, name="warm_out")
+
+        x_rows = x_words[0].rearrange("p c r -> p (c r)").bitcast(I32)
+        scale_rows = x_scales[0].bitcast(I32)
+        w_rows = w1.rearrange("(p j) c -> p j c", j=PACK)
+
+        nc.vector.memset(x_plane[:].bitcast(I32), 0)
+        nc.gpsimd.memset(warm_in[:], 0.0)
+        nc.scalar.activation(warm_out[:], warm_in[:], SIGMOID)
+
+        def load_weights(b):
+            nc.sync.dma_start(w_raw[b][:], w_rows[:, :, b * P : (b + 1) * P])
+
+        def load_store(b):
+            nc.sync.dma_start(store[b][:], mem[b * P : (b + 1) * P, :])
+
+        def load_updates(h):
+            nc.sync.dma_start(x_codes[h][:].bitcast(I32), x_rows[:, h * HALF : (h + 1) * HALF])
+
+        def quantize_weights(b):
+            nc.vector.quantize_mx(
+                out=w_codes[b][:].bitcast(FP8X4),
+                scales=w_plane[b][:],
+                in_=w_grouped[b][:].rearrange("p c j -> p (c j)"),
+            )
+
+        def make_gate(b, h):
+            cols = slice(h * HALF, (h + 1) * HALF)
+            acc = psum.tile([P, HALF], F32, name="acc%d%d" % (b, h))
+            nc.tensor.matmul_mx(
+                out=acc[:],
+                lhsT=w_codes[b][:].bitcast(FP8X4),
+                lhsT_scale=w_plane[b][:],
+                rhs=x_codes[h][:].bitcast(FP8X4),
+                rhs_scale=x_plane[:, cols],
+                start=True,
+                stop=True,
+            )
+            nc.scalar.activation(gate[b][:, cols], acc[:], SIGMOID)
+
+        def look_up(b):
+            nc.vector.tensor_copy(old[b][:], store[b][:].indirect(offsets[:]))
+
+        def put_back(b, first, last):
+            cols = slice(first, last)
+            entries = offsets[:, first // LIST_ROWS : last // LIST_ROWS]
+            nc.vector.tensor_tensor(store[b][:].indirect(entries), old[b][:, cols], gate[b][:, cols], MULT)
+
+        load_weights(0)
+        nc.sync.dma_start(offsets[:], slot)
+        load_store(0)
+        load_updates(0)
+        for r in range(4):
+            nc.sync.dma_start(x_plane[r:P:32, :].bitcast(I32), scale_rows[r:16:4, :])
+        load_store(1)
+        load_weights(1)
+        load_updates(1)
+
+        nc.vector.tensor_copy(w_grouped[0][:], w_raw[0][:].rearrange("p j c -> p c j"))
+        quantize_weights(0)
+        look_up(0)
+        make_gate(0, 0)
+        put_back(0, 0, HALF)
+        look_up(1)
+        nc.scalar.copy(w_grouped[1][:], w_raw[1][:].rearrange("p j c -> p c j"))
+        quantize_weights(1)
+        make_gate(0, 1)
+        put_back(0, HALF, T)
+        nc.sync.dma_start(out[0:P, :], store[0][:])
+        make_gate(1, 0)
+        make_gate(1, 1)
+        put_back(1, 0, T)
+        nc.sync.dma_start(out[P : 2 * P, :], store[1][:])

@@ -19,6 +19,7 @@ P = 128
 PACK = 4
 HALF = 512
 LIST_ROWS = 16
+FIRST = 256
 
 
 def tile_picked_widxput_gate_l_kernel(tc, x_words, x_scales, mem, w1, slot, out):
@@ -29,13 +30,14 @@ def tile_picked_widxput_gate_l_kernel(tc, x_words, x_scales, mem, w1, slot, out)
 
         offsets = keep.tile([P, T // LIST_ROWS], U16, name="offsets")
         x_plane = keep.tile([P, T], U8, name="x_plane", align_bytes=64)
-        x_codes = [keep.tile([P, HALF], U32, name="x_codes%d" % h, align_bytes=64) for h in range(2)]
-        w_raw = [keep.tile([P, PACK, P], F32, name="w_raw%d" % b, align_bytes=64) for b in range(2)]
+        x_first = keep.tile([P, FIRST], U32, name="x_first", align_bytes=64)
+        x_rest = keep.tile([P, T - FIRST], U32, name="x_rest", align_bytes=64)
+        old = [keep.tile([P, T], F32, name="old%d" % b, align_bytes=64) for b in range(2)]
+        w_raw = [keep.tile([P, PACK * P], F32, name="w_raw%d" % b, align_bytes=64)[:] for b in range(2)]
         w_grouped = [keep.tile([P, P, PACK], BF16, name="w_grouped%d" % b, align_bytes=64) for b in range(2)]
         w_codes = [keep.tile([P, P], U32, name="w_codes%d" % b, align_bytes=64) for b in range(2)]
         w_plane = [keep.tile([P, P], U8, name="w_plane%d" % b, align_bytes=64) for b in range(2)]
         store = [keep.tile([P, U], F32, name="store%d" % b, align_bytes=64) for b in range(2)]
-        old = [keep.tile([P, T], F32, name="old%d" % b, align_bytes=64) for b in range(2)]
         gate = [keep.tile([P, T], F32, name="gate%d" % b, align_bytes=64) for b in range(2)]
         warm_in = keep.tile([P, 8], F32, name="warm_in")
         warm_out = keep.tile([P, 8], F32, name="warm_out")
@@ -49,13 +51,13 @@ def tile_picked_widxput_gate_l_kernel(tc, x_words, x_scales, mem, w1, slot, out)
         nc.scalar.activation(warm_out[:], warm_in[:], SIGMOID)
 
         def load_weights(b):
-            nc.sync.dma_start(w_raw[b][:], w_rows[:, :, b * P : (b + 1) * P])
+            nc.sync.dma_start(w_raw[b].rearrange("p (j c) -> p j c", j=PACK), w_rows[:, :, b * P : (b + 1) * P])
 
         def load_store(b):
             nc.sync.dma_start(store[b][:], mem[b * P : (b + 1) * P, :])
 
-        def load_updates(h):
-            nc.sync.dma_start(x_codes[h][:].bitcast(I32), x_rows[:, h * HALF : (h + 1) * HALF])
+        def group_weights(b):
+            nc.scalar.copy(w_grouped[b][:], w_raw[b].rearrange("p (j c) -> p c j", j=PACK))
 
         def quantize_weights(b):
             nc.vector.quantize_mx(
@@ -64,50 +66,54 @@ def tile_picked_widxput_gate_l_kernel(tc, x_words, x_scales, mem, w1, slot, out)
                 in_=w_grouped[b][:].rearrange("p c j -> p (c j)"),
             )
 
-        def make_gate(b, h):
-            cols = slice(h * HALF, (h + 1) * HALF)
-            acc = psum.tile([P, HALF], F32, name="acc%d%d" % (b, h))
+        def make_gate(b, first, last):
+            codes = x_first[:] if first == 0 else x_rest[:, first - FIRST : last - FIRST]
+            acc = psum.tile([P, last - first], F32, name="acc%d_%d" % (b, first))
             nc.tensor.matmul_mx(
                 out=acc[:],
                 lhsT=w_codes[b][:].bitcast(FP8X4),
                 lhsT_scale=w_plane[b][:],
-                rhs=x_codes[h][:].bitcast(FP8X4),
-                rhs_scale=x_plane[:, cols],
+                rhs=codes.bitcast(FP8X4),
+                rhs_scale=x_plane[:, first:last],
                 start=True,
                 stop=True,
             )
-            nc.scalar.activation(gate[b][:, cols], acc[:], SIGMOID)
+            nc.scalar.activation(gate[b][:, first:last], acc[:], SIGMOID)
 
-        def look_up(b):
-            nc.vector.tensor_copy(old[b][:], store[b][:].indirect(offsets[:]))
+        def entries(first, last):
+            return offsets[:, first // LIST_ROWS : last // LIST_ROWS]
+
+        def look_up(b, first, last):
+            nc.vector.tensor_copy(old[b][:, first:last], store[b][:].indirect(entries(first, last)))
 
         def put_back(b, first, last):
             cols = slice(first, last)
-            entries = offsets[:, first // LIST_ROWS : last // LIST_ROWS]
-            nc.vector.tensor_tensor(store[b][:].indirect(entries), old[b][:, cols], gate[b][:, cols], MULT)
+            nc.vector.tensor_tensor(store[b][:].indirect(entries(first, last)), old[b][:, cols], gate[b][:, cols], MULT)
 
         load_weights(0)
         nc.sync.dma_start(offsets[:], slot)
         load_store(0)
-        load_updates(0)
+        load_weights(1)
+        nc.sync.dma_start(x_first[:].bitcast(I32), x_rows[:, 0:FIRST])
         for r in range(4):
             nc.sync.dma_start(x_plane[r:P:32, :].bitcast(I32), scale_rows[r:16:4, :])
         load_store(1)
-        load_weights(1)
-        load_updates(1)
+        nc.sync.dma_start(x_rest[:].bitcast(I32), x_rows[:, FIRST:T])
 
-        nc.vector.tensor_copy(w_grouped[0][:], w_raw[0][:].rearrange("p j c -> p c j"))
+        nc.vector.tensor_copy(w_grouped[0][:], w_raw[0].rearrange("p (j c) -> p c j", j=PACK))
         quantize_weights(0)
-        look_up(0)
-        make_gate(0, 0)
-        put_back(0, 0, HALF)
-        look_up(1)
-        nc.scalar.copy(w_grouped[1][:], w_raw[1][:].rearrange("p j c -> p c j"))
+        look_up(0, 0, T)
+        group_weights(1)
         quantize_weights(1)
-        make_gate(0, 1)
-        put_back(0, HALF, T)
+        make_gate(0, 0, FIRST)
+        put_back(0, 0, FIRST)
+        make_gate(0, FIRST, HALF)
+        make_gate(0, HALF, T)
+        make_gate(1, 0, FIRST)
+        make_gate(1, FIRST, HALF)
+        make_gate(1, HALF, T)
+        look_up(1, 0, T)
+        put_back(0, FIRST, T)
         nc.sync.dma_start(out[0:P, :], store[0][:])
-        make_gate(1, 0)
-        make_gate(1, 1)
         put_back(1, 0, T)
         nc.sync.dma_start(out[P : 2 * P, :], store[1][:])

@@ -30,8 +30,7 @@ def tile_picked_widxput_gate_l_kernel(tc, x_words, x_scales, mem, w1, slot, out)
 
         offsets = keep.tile([P, T // LIST_ROWS], U16, name="offsets")
         x_plane = keep.tile([P, T], U8, name="x_plane", align_bytes=64)
-        x_first = keep.tile([P, FIRST], U32, name="x_first", align_bytes=64)
-        x_rest = keep.tile([P, T - FIRST], U32, name="x_rest", align_bytes=64)
+        x_codes = keep.tile([P, T], U32, name="x_codes", align_bytes=64)
         old = [keep.tile([P, T], F32, name="old%d" % b, align_bytes=64) for b in range(2)]
         w_raw = [keep.tile([P, PACK * P], F32, name="w_raw%d" % b, align_bytes=64)[:] for b in range(2)]
         w_grouped = [keep.tile([P, P, PACK], BF16, name="w_grouped%d" % b, align_bytes=64) for b in range(2)]
@@ -56,6 +55,9 @@ def tile_picked_widxput_gate_l_kernel(tc, x_words, x_scales, mem, w1, slot, out)
         def load_store(b):
             nc.sync.dma_start(store[b][:], mem[b * P : (b + 1) * P, :])
 
+        def load_updates(first, last):
+            nc.sync.dma_start(x_codes[:, first:last].bitcast(I32), x_rows[:, first:last])
+
         def group_weights(b):
             nc.scalar.copy(w_grouped[b][:], w_raw[b].rearrange("p (j c) -> p c j", j=PACK))
 
@@ -67,13 +69,12 @@ def tile_picked_widxput_gate_l_kernel(tc, x_words, x_scales, mem, w1, slot, out)
             )
 
         def make_gate(b, first, last):
-            codes = x_first[:] if first == 0 else x_rest[:, first - FIRST : last - FIRST]
             acc = psum.tile([P, last - first], F32, name="acc%d_%d" % (b, first))
             nc.tensor.matmul_mx(
                 out=acc[:],
                 lhsT=w_codes[b][:].bitcast(FP8X4),
                 lhsT_scale=w_plane[b][:],
-                rhs=codes.bitcast(FP8X4),
+                rhs=x_codes[:, first:last].bitcast(FP8X4),
                 rhs_scale=x_plane[:, first:last],
                 start=True,
                 stop=True,
@@ -94,11 +95,12 @@ def tile_picked_widxput_gate_l_kernel(tc, x_words, x_scales, mem, w1, slot, out)
         nc.sync.dma_start(offsets[:], slot)
         load_store(0)
         load_weights(1)
-        nc.sync.dma_start(x_first[:].bitcast(I32), x_rows[:, 0:FIRST])
+        load_updates(0, FIRST)
         for r in range(4):
             nc.sync.dma_start(x_plane[r:P:32, :].bitcast(I32), scale_rows[r:16:4, :])
         load_store(1)
-        nc.sync.dma_start(x_rest[:].bitcast(I32), x_rows[:, FIRST:T])
+        load_updates(FIRST, HALF)
+        load_updates(HALF, T)
 
         nc.vector.tensor_copy(w_grouped[0][:], w_raw[0].rearrange("p (j c) -> p c j", j=PACK))
         quantize_weights(0)
@@ -107,13 +109,13 @@ def tile_picked_widxput_gate_l_kernel(tc, x_words, x_scales, mem, w1, slot, out)
         quantize_weights(1)
         make_gate(0, 0, FIRST)
         put_back(0, 0, FIRST)
-        make_gate(0, FIRST, HALF)
-        make_gate(0, HALF, T)
-        make_gate(1, 0, FIRST)
-        make_gate(1, FIRST, HALF)
-        make_gate(1, HALF, T)
         look_up(1, 0, T)
-        put_back(0, FIRST, T)
-        nc.sync.dma_start(out[0:P, :], store[0][:])
+        make_gate(0, FIRST, HALF)
+        put_back(0, FIRST, HALF)
+        make_gate(1, 0, HALF)
+        make_gate(1, HALF, T)
         put_back(1, 0, T)
         nc.sync.dma_start(out[P : 2 * P, :], store[1][:])
+        make_gate(0, HALF, T)
+        put_back(0, HALF, T)
+        nc.sync.dma_start(out[0:P, :], store[0][:])

@@ -29,7 +29,7 @@ def tile_picked_widxput_gate_l_kernel(tc, x_words, x_scales, mem, w1, slot, out)
         psum = ctx.enter_context(tc.psum_pool(name="psum", bufs=1))
 
         offsets = keep.tile([P, T // LIST_ROWS], U16, name="offsets")
-        x_plane = keep.tile([P, T], U8, name="x_plane", align_bytes=64)
+        x_plane = keep.tile([P, FIRST], U8, name="x_plane", align_bytes=64)
         x_codes = keep.tile([P, T], U32, name="x_codes", align_bytes=64)
         old = [keep.tile([P, T], F32, name="old%d" % b, align_bytes=64) for b in range(2)]
         w_raw = [keep.tile([P, PACK * P], F32, name="w_raw%d" % b, align_bytes=64)[:] for b in range(2)]
@@ -70,15 +70,17 @@ def tile_picked_widxput_gate_l_kernel(tc, x_words, x_scales, mem, w1, slot, out)
 
         def make_gate(b, first, last):
             acc = psum.tile([P, last - first], F32, name="acc%d_%d" % (b, first))
-            nc.tensor.matmul_mx(
-                out=acc[:],
-                lhsT=w_codes[b][:].bitcast(FP8X4),
-                lhsT_scale=w_plane[b][:],
-                rhs=x_codes[:, first:last].bitcast(FP8X4),
-                rhs_scale=x_plane[:, first:last],
-                start=True,
-                stop=True,
-            )
+            step = min(FIRST, last - first)
+            for c in range(first, last, step):
+                nc.tensor.matmul_mx(
+                    out=acc[:, c - first : c - first + step],
+                    lhsT=w_codes[b][:].bitcast(FP8X4),
+                    lhsT_scale=w_plane[b][:],
+                    rhs=x_codes[:, c : c + step].bitcast(FP8X4),
+                    rhs_scale=x_plane[4 * (c // FIRST) : P, c % FIRST : c % FIRST + step],
+                    start=True,
+                    stop=True,
+                )
             nc.scalar.activation(gate[b][:, first:last], acc[:], SIGMOID)
 
         def entries(first, last):
@@ -96,8 +98,11 @@ def tile_picked_widxput_gate_l_kernel(tc, x_words, x_scales, mem, w1, slot, out)
         load_store(0)
         load_weights(1)
         load_updates(0, FIRST)
-        for r in range(4):
-            nc.sync.dma_start(x_plane[r:P:32, :].bitcast(I32), scale_rows[r:16:4, :])
+        for q in range(4):
+            nc.sync.dma_start(
+                x_plane[32 * q : 32 * q + 16, :].bitcast(I32),
+                scale_rows[4 * q : 4 * q + 4, :].rearrange("r (a c) -> a r c", a=4),
+            )
         load_store(1)
         load_updates(FIRST, HALF)
         load_updates(HALF, T)
@@ -107,7 +112,8 @@ def tile_picked_widxput_gate_l_kernel(tc, x_words, x_scales, mem, w1, slot, out)
         look_up(0, 0, T)
         group_weights(1)
         quantize_weights(1)
-        make_gate(0, 0, FIRST)
+        make_gate(0, 0, FIRST // 2)
+        make_gate(0, FIRST // 2, FIRST)
         put_back(0, 0, FIRST)
         look_up(1, 0, T)
         make_gate(0, FIRST, HALF)

@@ -17,9 +17,13 @@ MULT = mybir.AluOpType.mult
 
 P = 128
 PACK = 4
-HALF = 512
 LIST_ROWS = 16
-FIRST = 256
+QUADRANT = 32
+SCALE_ROWS = 4
+QUARTERS = 4
+QUARTER = T // QUARTERS
+HALF = T // 2
+WARM_COLUMNS = 8
 
 
 def tile_picked_widxput_gate_l_kernel(tc, x_words, x_scales, mem, w1, slot, out):
@@ -29,25 +33,22 @@ def tile_picked_widxput_gate_l_kernel(tc, x_words, x_scales, mem, w1, slot, out)
         psum = ctx.enter_context(tc.psum_pool(name="psum", bufs=1))
 
         offsets = keep.tile([P, T // LIST_ROWS], U16, name="offsets")
-        x_plane = keep.tile([P, FIRST], U8, name="x_plane", align_bytes=64)
+        x_scale = keep.tile([P, QUARTER], U8, name="x_scale", align_bytes=64)
         x_codes = keep.tile([P, T], U32, name="x_codes", align_bytes=64)
         old = [keep.tile([P, T], F32, name="old%d" % b, align_bytes=64) for b in range(2)]
         w_raw = [keep.tile([P, PACK * P], F32, name="w_raw%d" % b, align_bytes=64)[:] for b in range(2)]
         w_grouped = [keep.tile([P, P, PACK], BF16, name="w_grouped%d" % b, align_bytes=64) for b in range(2)]
         w_codes = [keep.tile([P, P], U32, name="w_codes%d" % b, align_bytes=64) for b in range(2)]
-        w_plane = [keep.tile([P, P], U8, name="w_plane%d" % b, align_bytes=64) for b in range(2)]
+        w_scale = [keep.tile([P, P], U8, name="w_scale%d" % b, align_bytes=64) for b in range(2)]
         store = [keep.tile([P, U], F32, name="store%d" % b, align_bytes=64) for b in range(2)]
         gate = [keep.tile([P, T], F32, name="gate%d" % b, align_bytes=64) for b in range(2)]
-        warm_in = keep.tile([P, 8], F32, name="warm_in")
-        warm_out = keep.tile([P, 8], F32, name="warm_out")
+        warm_out = keep.tile([P, WARM_COLUMNS], F32, name="warm_out")
 
         x_rows = x_words[0].rearrange("p c r -> p (c r)").bitcast(I32)
         scale_rows = x_scales[0].bitcast(I32)
         w_rows = w1.rearrange("(p j) c -> p j c", j=PACK)
 
-        nc.vector.memset(x_plane[:].bitcast(I32), 0)
-        nc.gpsimd.memset(warm_in[:], 0.0)
-        nc.scalar.activation(warm_out[:], warm_in[:], SIGMOID)
+        nc.vector.memset(x_scale[:].bitcast(I32), 0)
 
         def load_weights(b):
             nc.sync.dma_start(w_raw[b].rearrange("p (j c) -> p j c", j=PACK), w_rows[:, :, b * P : (b + 1) * P])
@@ -58,70 +59,72 @@ def tile_picked_widxput_gate_l_kernel(tc, x_words, x_scales, mem, w1, slot, out)
         def load_updates(first, last):
             nc.sync.dma_start(x_codes[:, first:last].bitcast(I32), x_rows[:, first:last])
 
-        def group_weights(b):
-            nc.scalar.copy(w_grouped[b][:], w_raw[b].rearrange("p (j c) -> p c j", j=PACK))
+        def group_weights(copy, b):
+            copy(w_grouped[b][:], w_raw[b].rearrange("p (j c) -> p c j", j=PACK))
 
         def quantize_weights(b):
             nc.vector.quantize_mx(
                 out=w_codes[b][:].bitcast(FP8X4),
-                scales=w_plane[b][:],
+                scales=w_scale[b][:],
                 in_=w_grouped[b][:].rearrange("p c j -> p (c j)"),
             )
 
-        def make_gate(b, first, last):
-            acc = psum.tile([P, last - first], F32, name="acc%d_%d" % (b, first))
-            step = min(FIRST, last - first)
-            for c in range(first, last, step):
-                nc.tensor.matmul_mx(
-                    out=acc[:, c - first : c - first + step],
-                    lhsT=w_codes[b][:].bitcast(FP8X4),
-                    lhsT_scale=w_plane[b][:],
-                    rhs=x_codes[:, c : c + step].bitcast(FP8X4),
-                    rhs_scale=x_plane[4 * (c // FIRST) : P, c % FIRST : c % FIRST + step],
-                    start=True,
-                    stop=True,
-                )
+        def make_gate(b, first, last, bank):
+            acc = psum.tile([P, last - first], F32, name="bank%d" % bank)
+            nc.tensor.matmul_mx(
+                out=acc[:],
+                lhsT=w_codes[b][:].bitcast(FP8X4),
+                lhsT_scale=w_scale[b][:],
+                rhs=x_codes[:, first:last].bitcast(FP8X4),
+                rhs_scale=x_scale[SCALE_ROWS * (first // QUARTER) : P, first % QUARTER : first % QUARTER + last - first],
+                start=True,
+                stop=True,
+            )
             nc.scalar.activation(gate[b][:, first:last], acc[:], SIGMOID)
 
         def entries(first, last):
             return offsets[:, first // LIST_ROWS : last // LIST_ROWS]
 
-        def look_up(b, first, last):
-            nc.vector.tensor_copy(old[b][:, first:last], store[b][:].indirect(entries(first, last)))
+        def look_up(b):
+            nc.vector.tensor_copy(old[b][:], store[b][:].indirect(entries(0, T)))
 
         def put_back(b, first, last):
             cols = slice(first, last)
             nc.vector.tensor_tensor(store[b][:].indirect(entries(first, last)), old[b][:, cols], gate[b][:, cols], MULT)
 
         load_weights(0)
+        nc.scalar.activation(warm_out[:], w_raw[0][:, 0:WARM_COLUMNS], SIGMOID)
         nc.sync.dma_start(offsets[:], slot)
         load_store(0)
         load_weights(1)
-        load_updates(0, FIRST)
-        for q in range(4):
+        load_updates(0, QUARTER)
+        for q in range(P // QUADRANT):
             nc.sync.dma_start(
-                x_plane[32 * q : 32 * q + 16, :].bitcast(I32),
-                scale_rows[4 * q : 4 * q + 4, :].rearrange("r (a c) -> a r c", a=4),
+                x_scale[QUADRANT * q : QUADRANT * q + QUARTERS * SCALE_ROWS, :].bitcast(I32),
+                scale_rows[SCALE_ROWS * q : SCALE_ROWS * (q + 1), :].rearrange("r (a c) -> a r c", a=QUARTERS),
             )
         load_store(1)
-        load_updates(FIRST, HALF)
+        load_updates(QUARTER, HALF)
         load_updates(HALF, T)
 
-        nc.vector.tensor_copy(w_grouped[0][:], w_raw[0].rearrange("p (j c) -> p c j", j=PACK))
+        group_weights(nc.vector.tensor_copy, 0)
         quantize_weights(0)
-        look_up(0, 0, T)
-        group_weights(1)
+        look_up(0)
+        group_weights(nc.scalar.copy, 1)
         quantize_weights(1)
-        make_gate(0, 0, FIRST // 2)
-        make_gate(0, FIRST // 2, FIRST)
-        put_back(0, 0, FIRST)
-        look_up(1, 0, T)
-        make_gate(0, FIRST, HALF)
-        put_back(0, FIRST, HALF)
-        make_gate(1, 0, HALF)
-        make_gate(1, HALF, T)
+
+        make_gate(0, 0, QUARTER // 2, 0)
+        make_gate(0, QUARTER // 2, QUARTER, 1)
+        put_back(0, 0, QUARTER)
+        look_up(1)
+        make_gate(0, QUARTER, HALF, 2)
+        put_back(0, QUARTER, HALF)
+        for a in range(QUARTERS):
+            make_gate(1, a * QUARTER, (a + 1) * QUARTER, 3 + a)
         put_back(1, 0, T)
         nc.sync.dma_start(out[P : 2 * P, :], store[1][:])
-        make_gate(0, HALF, T)
+
+        for bank, first in enumerate(range(HALF, T, QUARTER)):
+            make_gate(0, first, first + QUARTER, bank)
         put_back(0, HALF, T)
         nc.sync.dma_start(out[0:P, :], store[0][:])

@@ -104,8 +104,8 @@ def tile_picked_widxput_gate_l_kernel(tc, x_words, x_scales, mem, w1, slot, out)
                 scale_rows[SCALE_ROWS * q : SCALE_ROWS * (q + 1), :].rearrange("r (a c) -> a r c", a=QUARTERS),
             )
         load_store(1)
-        load_updates(QUARTER, HALF)
-        load_updates(HALF, T)
+        for first in range(QUARTER, T, QUARTER):
+            load_updates(first, first + QUARTER)
 
         group_weights(nc.vector.tensor_copy, 0)
         quantize_weights(0)
@@ -122,7 +122,8 @@ def tile_picked_widxput_gate_l_kernel(tc, x_words, x_scales, mem, w1, slot, out)
         for a in range(QUARTERS):
             make_gate(1, a * QUARTER, (a + 1) * QUARTER, 3 + a)
         put_back(1, 0, T)
-        nc.sync.dma_start(out[P : 2 * P, :], store[1][:])
+        for cols in (slice(0, U // 2), slice(U // 2, U)):
+            nc.sync.dma_start(out[P : 2 * P, cols], store[1][:, cols])
 
         for bank, first in enumerate(range(HALF, T, QUARTER)):
             make_gate(0, first, first + QUARTER, bank)

@@ -13,6 +13,7 @@ U16 = mybir.dt.uint16
 U8 = mybir.dt.uint8
 FP8X4 = mybir.dt.float8_e4m3fn_x4
 SIGMOID = mybir.ActivationFunctionType.Sigmoid
+COPY = mybir.ActivationFunctionType.Copy
 MULT = mybir.AluOpType.mult
 
 P = 128
@@ -22,8 +23,12 @@ QUADRANT = 32
 SCALE_ROWS = 4
 QUARTERS = 4
 QUARTER = T // QUARTERS
-HALF = T // 2
-WARM_COLUMNS = 8
+EARLY = 128
+LATE = T - 128
+A_GATHER = 608
+A_FIRST = 256
+B_FUSED = 384
+B_SCALAR = 736
 
 
 def tile_picked_widxput_gate_l_kernel(tc, x_words, x_scales, mem, w1, slot, out):
@@ -36,22 +41,19 @@ def tile_picked_widxput_gate_l_kernel(tc, x_words, x_scales, mem, w1, slot, out)
         x_scale = keep.tile([P, QUARTER], U8, name="x_scale", align_bytes=64)
         x_codes = keep.tile([P, T], U32, name="x_codes", align_bytes=64)
         old = [keep.tile([P, T], F32, name="old%d" % b, align_bytes=64) for b in range(2)]
-        w_raw = [keep.tile([P, PACK * P], F32, name="w_raw%d" % b, align_bytes=64)[:] for b in range(2)]
+        w_raw = keep.tile([P, PACK, N], F32, name="w_raw", align_bytes=64)
         w_grouped = [keep.tile([P, P, PACK], BF16, name="w_grouped%d" % b, align_bytes=64) for b in range(2)]
         w_codes = [keep.tile([P, P], U32, name="w_codes%d" % b, align_bytes=64) for b in range(2)]
         w_scale = [keep.tile([P, P], U8, name="w_scale%d" % b, align_bytes=64) for b in range(2)]
         store = [keep.tile([P, U], F32, name="store%d" % b, align_bytes=64) for b in range(2)]
         gate = [keep.tile([P, T], F32, name="gate%d" % b, align_bytes=64) for b in range(2)]
-        warm_out = keep.tile([P, WARM_COLUMNS], F32, name="warm_out")
+        fresh = keep.tile([P, B_SCALAR - B_FUSED], F32, name="fresh", align_bytes=64)
+        fused = keep.tile([P, B_FUSED], F32, name="fused", align_bytes=64)[:]
 
         x_rows = x_words[0].rearrange("p c r -> p (c r)").bitcast(I32)
         scale_rows = x_scales[0].bitcast(I32)
-        w_rows = w1.rearrange("(p j) c -> p j c", j=PACK)
 
         nc.vector.memset(x_scale[:].bitcast(I32), 0)
-
-        def load_weights(b):
-            nc.sync.dma_start(w_raw[b].rearrange("p (j c) -> p j c", j=PACK), w_rows[:, :, b * P : (b + 1) * P])
 
         def load_store(b):
             nc.sync.dma_start(store[b][:], mem[b * P : (b + 1) * P, :])
@@ -59,8 +61,8 @@ def tile_picked_widxput_gate_l_kernel(tc, x_words, x_scales, mem, w1, slot, out)
         def load_updates(first, last):
             nc.sync.dma_start(x_codes[:, first:last].bitcast(I32), x_rows[:, first:last])
 
-        def group_weights(copy, b):
-            copy(w_grouped[b][:], w_raw[b].rearrange("p (j c) -> p c j", j=PACK))
+        def group_weights(b):
+            nc.vector.tensor_copy(w_grouped[b][:], w_raw[:, :, b * P : (b + 1) * P].rearrange("p j c -> p c j"))
 
         def quantize_weights(b):
             nc.vector.quantize_mx(
@@ -70,62 +72,63 @@ def tile_picked_widxput_gate_l_kernel(tc, x_words, x_scales, mem, w1, slot, out)
             )
 
         def make_gate(b, first, last, bank):
+            cols = slice(first, last)
             acc = psum.tile([P, last - first], F32, name="bank%d" % bank)
             nc.tensor.matmul_mx(
                 out=acc[:],
                 lhsT=w_codes[b][:].bitcast(FP8X4),
                 lhsT_scale=w_scale[b][:],
-                rhs=x_codes[:, first:last].bitcast(FP8X4),
+                rhs=x_codes[:, cols].bitcast(FP8X4),
                 rhs_scale=x_scale[SCALE_ROWS * (first // QUARTER) : P, first % QUARTER : first % QUARTER + last - first],
                 start=True,
                 stop=True,
             )
-            nc.scalar.activation(gate[b][:, first:last], acc[:], SIGMOID)
+            nc.scalar.activation(gate[b][:, cols], acc[:], SIGMOID)
 
-        def entries(first, last):
-            return offsets[:, first // LIST_ROWS : last // LIST_ROWS]
+        def listed(b, first, last):
+            return store[b][:].indirect(offsets[:, first // LIST_ROWS : last // LIST_ROWS])
 
-        def look_up(b):
-            nc.vector.tensor_copy(old[b][:], store[b][:].indirect(entries(0, T)))
+        def load_scales():
+            for q in range(P // QUADRANT):
+                nc.sync.dma_start(
+                    x_scale[QUADRANT * q : QUADRANT * q + QUARTERS * SCALE_ROWS, :].bitcast(I32),
+                    scale_rows[SCALE_ROWS * q : SCALE_ROWS * (q + 1), :].rearrange("r (a c) -> a r c", a=QUARTERS),
+                )
 
-        def put_back(b, first, last):
-            cols = slice(first, last)
-            nc.vector.tensor_tensor(store[b][:].indirect(entries(first, last)), old[b][:, cols], gate[b][:, cols], MULT)
+        def put_product(b, first, last):
+            nc.vector.tensor_tensor(listed(b, first, last), old[b][:, first:last], gate[b][:, first:last], MULT)
 
-        load_weights(0)
-        nc.scalar.activation(warm_out[:], w_raw[0][:, 0:WARM_COLUMNS], SIGMOID)
+        nc.sync.dma_start(w_raw[:], w1.rearrange("(p j) c -> p j c", j=PACK))
         nc.sync.dma_start(offsets[:], slot)
+        load_scales()
+        load_updates(0, EARLY)
         load_store(0)
-        load_weights(1)
-        load_updates(0, QUARTER)
-        for q in range(P // QUADRANT):
-            nc.sync.dma_start(
-                x_scale[QUADRANT * q : QUADRANT * q + QUARTERS * SCALE_ROWS, :].bitcast(I32),
-                scale_rows[SCALE_ROWS * q : SCALE_ROWS * (q + 1), :].rearrange("r (a c) -> a r c", a=QUARTERS),
-            )
+        load_updates(EARLY, LATE)
         load_store(1)
-        for first in range(QUARTER, T, QUARTER):
-            load_updates(first, first + QUARTER)
+        load_updates(LATE, T)
 
-        group_weights(nc.vector.tensor_copy, 0)
-        quantize_weights(0)
-        look_up(0)
-        group_weights(nc.scalar.copy, 1)
-        quantize_weights(1)
+        for b in range(2):
+            group_weights(b)
+        for b in range(2):
+            quantize_weights(b)
+        for b in range(2):
+            make_gate(b, 0, EARLY, b)
 
-        make_gate(0, 0, QUARTER // 2, 0)
-        make_gate(0, QUARTER // 2, QUARTER, 1)
-        put_back(0, 0, QUARTER)
-        look_up(1)
-        make_gate(0, QUARTER, HALF, 2)
-        put_back(0, QUARTER, HALF)
-        for a in range(QUARTERS):
-            make_gate(1, a * QUARTER, (a + 1) * QUARTER, 3 + a)
-        put_back(1, 0, T)
-        for cols in (slice(0, U // 2), slice(U // 2, U)):
-            nc.sync.dma_start(out[P : 2 * P, cols], store[1][:, cols])
-
-        for bank, first in enumerate(range(HALF, T, QUARTER)):
-            make_gate(0, first, first + QUARTER, bank)
-        put_back(0, HALF, T)
+        nc.vector.tensor_copy(old[0][:, 0:A_GATHER], listed(0, 0, A_GATHER))
+        nc.scalar.activation(old[0][:, A_GATHER:T], listed(0, A_GATHER, T), COPY)
+        cuts = [EARLY, QUARTER, 2 * QUARTER, 3 * QUARTER, LATE]
+        for b in range(2):
+            for i in range(4):
+                make_gate(b, cuts[i], cuts[i + 1], (2 + 4 * b + i) % 8)
+        put_product(0, 0, A_FIRST)
+        nc.scalar.activation(old[1][:, B_FUSED:T], listed(1, B_FUSED, T), COPY)
+        nc.vector.tensor_tensor(fused, listed(1, 0, B_FUSED), gate[1][:, 0:B_FUSED], MULT)
+        nc.vector.tensor_tensor(fresh[:], old[1][:, B_FUSED:B_SCALAR], gate[1][:, B_FUSED:B_SCALAR], MULT)
+        make_gate(0, LATE, T, 2)
+        nc.scalar.activation(listed(1, 0, B_FUSED), fused, COPY)
+        put_product(0, A_FIRST, T)
         nc.sync.dma_start(out[0:P, :], store[0][:])
+        make_gate(1, LATE, T, 2)
+        nc.scalar.activation(listed(1, B_FUSED, B_SCALAR), fresh[:], COPY)
+        put_product(1, B_SCALAR, T)
+        nc.sync.dma_start(out[P : 2 * P, :], store[1][:])

@@ -23,12 +23,13 @@ QUADRANT = 32
 SCALE_ROWS = 4
 QUARTERS = 4
 QUARTER = T // QUARTERS
-EARLY = 128
 LATE = T - 128
-A_GATHER = 608
+A_GATHER = 576
 A_FIRST = 256
-B_FUSED = 384
-B_SCALAR = 736
+B_FUSED = 448
+B_CUT = 384
+B_SCALAR = 704
+WARM_COLUMNS = 8
 
 
 def tile_picked_widxput_gate_l_kernel(tc, x_words, x_scales, mem, w1, slot, out):
@@ -47,8 +48,8 @@ def tile_picked_widxput_gate_l_kernel(tc, x_words, x_scales, mem, w1, slot, out)
         w_scale = [keep.tile([P, P], U8, name="w_scale%d" % b, align_bytes=64) for b in range(2)]
         store = [keep.tile([P, U], F32, name="store%d" % b, align_bytes=64) for b in range(2)]
         gate = [keep.tile([P, T], F32, name="gate%d" % b, align_bytes=64) for b in range(2)]
-        fresh = keep.tile([P, B_SCALAR - B_FUSED], F32, name="fresh", align_bytes=64)
-        fused = keep.tile([P, B_FUSED], F32, name="fused", align_bytes=64)[:]
+        fresh = keep.tile([P, B_SCALAR], F32, name="fresh", align_bytes=64)
+        warm_out = keep.tile([P, WARM_COLUMNS], F32, name="warm_out")
 
         x_rows = x_words[0].rearrange("p c r -> p (c r)").bitcast(I32)
         scale_rows = x_scales[0].bitcast(I32)
@@ -99,11 +100,12 @@ def tile_picked_widxput_gate_l_kernel(tc, x_words, x_scales, mem, w1, slot, out)
             nc.vector.tensor_tensor(listed(b, first, last), old[b][:, first:last], gate[b][:, first:last], MULT)
 
         nc.sync.dma_start(w_raw[:], w1.rearrange("(p j) c -> p j c", j=PACK))
+        nc.scalar.activation(warm_out[:], w_raw[:, 0, 0:WARM_COLUMNS], SIGMOID)
         nc.sync.dma_start(offsets[:], slot)
-        load_scales()
-        load_updates(0, EARLY)
         load_store(0)
-        load_updates(EARLY, LATE)
+        load_scales()
+        load_updates(0, QUARTER)
+        load_updates(QUARTER, LATE)
         load_store(1)
         load_updates(LATE, T)
 
@@ -111,24 +113,22 @@ def tile_picked_widxput_gate_l_kernel(tc, x_words, x_scales, mem, w1, slot, out)
             group_weights(b)
         for b in range(2):
             quantize_weights(b)
-        for b in range(2):
-            make_gate(b, 0, EARLY, b)
 
         nc.vector.tensor_copy(old[0][:, 0:A_GATHER], listed(0, 0, A_GATHER))
         nc.scalar.activation(old[0][:, A_GATHER:T], listed(0, A_GATHER, T), COPY)
-        cuts = [EARLY, QUARTER, 2 * QUARTER, 3 * QUARTER, LATE]
+        cuts = [0, QUARTER, 2 * QUARTER, 3 * QUARTER, LATE]
         for b in range(2):
             for i in range(4):
-                make_gate(b, cuts[i], cuts[i + 1], (2 + 4 * b + i) % 8)
+                make_gate(b, cuts[i], cuts[i + 1], 4 * b + i)
         put_product(0, 0, A_FIRST)
         nc.scalar.activation(old[1][:, B_FUSED:T], listed(1, B_FUSED, T), COPY)
-        nc.vector.tensor_tensor(fused, listed(1, 0, B_FUSED), gate[1][:, 0:B_FUSED], MULT)
-        nc.vector.tensor_tensor(fresh[:], old[1][:, B_FUSED:B_SCALAR], gate[1][:, B_FUSED:B_SCALAR], MULT)
-        make_gate(0, LATE, T, 2)
-        nc.scalar.activation(listed(1, 0, B_FUSED), fused, COPY)
+        nc.vector.tensor_tensor(fresh[:, 0:B_FUSED], listed(1, 0, B_FUSED), gate[1][:, 0:B_FUSED], MULT)
+        nc.vector.tensor_tensor(fresh[:, B_FUSED:B_SCALAR], old[1][:, B_FUSED:B_SCALAR], gate[1][:, B_FUSED:B_SCALAR], MULT)
+        make_gate(0, LATE, T, 0)
+        nc.scalar.activation(listed(1, 0, B_CUT), fresh[:, 0:B_CUT], COPY)
         put_product(0, A_FIRST, T)
         nc.sync.dma_start(out[0:P, :], store[0][:])
-        make_gate(1, LATE, T, 2)
-        nc.scalar.activation(listed(1, B_FUSED, B_SCALAR), fresh[:], COPY)
+        make_gate(1, LATE, T, 0)
+        nc.scalar.activation(listed(1, B_CUT, B_SCALAR), fresh[:, B_CUT:B_SCALAR], COPY)
         put_product(1, B_SCALAR, T)
         nc.sync.dma_start(out[P : 2 * P, :], store[1][:])

@@ -23,12 +23,10 @@ QUADRANT = 32
 SCALE_ROWS = 4
 QUARTERS = 4
 QUARTER = T // QUARTERS
-LATE = T - 128
 A_GATHER = 576
-A_FIRST = 256
-B_FUSED = 448
-B_CUT = 384
-B_SCALAR = 704
+A_VECTOR = QUARTER
+A_CUT = 640
+B_GATHER = 512
 WARM_COLUMNS = 8
 
 
@@ -48,7 +46,7 @@ def tile_picked_widxput_gate_l_kernel(tc, x_words, x_scales, mem, w1, slot, out)
         w_scale = [keep.tile([P, P], U8, name="w_scale%d" % b, align_bytes=64) for b in range(2)]
         store = [keep.tile([P, U], F32, name="store%d" % b, align_bytes=64) for b in range(2)]
         gate = [keep.tile([P, T], F32, name="gate%d" % b, align_bytes=64) for b in range(2)]
-        fresh = keep.tile([P, B_SCALAR], F32, name="fresh", align_bytes=64)
+        fresh = keep.tile([P, T], F32, name="fresh", align_bytes=64)
         warm_out = keep.tile([P, WARM_COLUMNS], F32, name="warm_out")
 
         x_rows = x_words[0].rearrange("p c r -> p (c r)").bitcast(I32)
@@ -105,9 +103,8 @@ def tile_picked_widxput_gate_l_kernel(tc, x_words, x_scales, mem, w1, slot, out)
         load_store(0)
         load_scales()
         load_updates(0, QUARTER)
-        load_updates(QUARTER, LATE)
+        load_updates(QUARTER, T)
         load_store(1)
-        load_updates(LATE, T)
 
         for b in range(2):
             group_weights(b)
@@ -116,19 +113,17 @@ def tile_picked_widxput_gate_l_kernel(tc, x_words, x_scales, mem, w1, slot, out)
 
         nc.vector.tensor_copy(old[0][:, 0:A_GATHER], listed(0, 0, A_GATHER))
         nc.scalar.activation(old[0][:, A_GATHER:T], listed(0, A_GATHER, T), COPY)
-        cuts = [0, QUARTER, 2 * QUARTER, 3 * QUARTER, LATE]
         for b in range(2):
-            for i in range(4):
-                make_gate(b, cuts[i], cuts[i + 1], 4 * b + i)
-        put_product(0, 0, A_FIRST)
-        nc.scalar.activation(old[1][:, B_FUSED:T], listed(1, B_FUSED, T), COPY)
-        nc.vector.tensor_tensor(fresh[:, 0:B_FUSED], listed(1, 0, B_FUSED), gate[1][:, 0:B_FUSED], MULT)
-        nc.vector.tensor_tensor(fresh[:, B_FUSED:B_SCALAR], old[1][:, B_FUSED:B_SCALAR], gate[1][:, B_FUSED:B_SCALAR], MULT)
-        make_gate(0, LATE, T, 0)
-        nc.scalar.activation(listed(1, 0, B_CUT), fresh[:, 0:B_CUT], COPY)
-        put_product(0, A_FIRST, T)
-        nc.sync.dma_start(out[0:P, :], store[0][:])
-        make_gate(1, LATE, T, 0)
-        nc.scalar.activation(listed(1, B_CUT, B_SCALAR), fresh[:, B_CUT:B_SCALAR], COPY)
-        put_product(1, B_SCALAR, T)
+            for a in range(QUARTERS - 1 + b):
+                make_gate(b, a * QUARTER, (a + 1) * QUARTER, QUARTERS * b + a)
+        make_gate(0, T - QUARTER, T, QUARTERS - 1)
+        put_product(0, 0, A_VECTOR)
+        for cols in (slice(A_VECTOR, A_CUT), slice(A_CUT, T)):
+            nc.vector.tensor_tensor(fresh[:, cols], old[0][:, cols], gate[0][:, cols], MULT)
+        nc.scalar.activation(old[1][:, 0:B_GATHER], listed(1, 0, B_GATHER), COPY)
+        nc.vector.tensor_copy(old[1][:, B_GATHER:T], listed(1, B_GATHER, T))
+        nc.scalar.activation(listed(0, A_CUT, T), fresh[:, A_CUT:T], COPY)
+        nc.scalar.activation(listed(0, A_VECTOR, A_CUT), fresh[:, A_VECTOR:A_CUT], COPY)
+        nc.scalar.dma_start(out[0:P, :], store[0][:])
+        put_product(1, 0, T)
         nc.sync.dma_start(out[P : 2 * P, :], store[1][:])

@@ -26,7 +26,7 @@ QUARTER = T // QUARTERS
 A_GATHER = 576
 A_VECTOR = QUARTER
 A_CUT = 640
-B_GATHER = 512
+B_GATHER = 640
 WARM_COLUMNS = 8
 
 
@@ -118,7 +118,7 @@ def tile_picked_widxput_gate_l_kernel(tc, x_words, x_scales, mem, w1, slot, out)
                 make_gate(b, a * QUARTER, (a + 1) * QUARTER, QUARTERS * b + a)
         make_gate(0, T - QUARTER, T, QUARTERS - 1)
         put_product(0, 0, A_VECTOR)
-        for cols in (slice(A_VECTOR, A_CUT), slice(A_CUT, T)):
+        for cols in (slice(A_VECTOR, T - QUARTER), slice(T - QUARTER, T)):
             nc.vector.tensor_tensor(fresh[:, cols], old[0][:, cols], gate[0][:, cols], MULT)
         nc.scalar.activation(old[1][:, 0:B_GATHER], listed(1, 0, B_GATHER), COPY)
         nc.vector.tensor_copy(old[1][:, B_GATHER:T], listed(1, B_GATHER, T))
@@ -126,4 +126,5 @@ def tile_picked_widxput_gate_l_kernel(tc, x_words, x_scales, mem, w1, slot, out)
         nc.scalar.activation(listed(0, A_VECTOR, A_CUT), fresh[:, A_VECTOR:A_CUT], COPY)
         nc.scalar.dma_start(out[0:P, :], store[0][:])
         put_product(1, 0, T)
-        nc.sync.dma_start(out[P : 2 * P, :], store[1][:])
+        for cols in (slice(0, U // 2), slice(U // 2, U)):
+            nc.sync.dma_start(out[P : 2 * P, cols], store[1][:, cols])

@@ -26,7 +26,7 @@ QUARTER = T // QUARTERS
 A_GATHER = 576
 A_VECTOR = QUARTER
 A_CUT = 640
-B_GATHER = 640
+B_GATHER = 576
 WARM_COLUMNS = 8
 
 
@@ -113,10 +113,12 @@ def tile_picked_widxput_gate_l_kernel(tc, x_words, x_scales, mem, w1, slot, out)
 
         nc.vector.tensor_copy(old[0][:, 0:A_GATHER], listed(0, 0, A_GATHER))
         nc.scalar.activation(old[0][:, A_GATHER:T], listed(0, A_GATHER, T), COPY)
+        make_gate(0, 0, QUARTER // 2, 0)
+        make_gate(0, QUARTER // 2, QUARTER, 1)
         for b in range(2):
-            for a in range(QUARTERS - 1 + b):
-                make_gate(b, a * QUARTER, (a + 1) * QUARTER, QUARTERS * b + a)
-        make_gate(0, T - QUARTER, T, QUARTERS - 1)
+            for a in range(1 - b, QUARTERS - 1 + b):
+                make_gate(b, a * QUARTER, (a + 1) * QUARTER, 1 + 3 * b + a)
+        make_gate(0, T - QUARTER, T, 0)
         put_product(0, 0, A_VECTOR)
         for cols in (slice(A_VECTOR, T - QUARTER), slice(T - QUARTER, T)):
             nc.vector.tensor_tensor(fresh[:, cols], old[0][:, cols], gate[0][:, cols], MULT)

@@ -23,11 +23,10 @@ QUADRANT = 32
 SCALE_ROWS = 4
 QUARTERS = 4
 QUARTER = T // QUARTERS
-A_GATHER = 576
+A_GATHER = 512
 A_VECTOR = QUARTER
 A_CUT = 640
-B_GATHER = 576
-WARM_COLUMNS = 8
+B_GATHER = 544
 
 
 def tile_picked_widxput_gate_l_kernel(tc, x_words, x_scales, mem, w1, slot, out):
@@ -47,7 +46,6 @@ def tile_picked_widxput_gate_l_kernel(tc, x_words, x_scales, mem, w1, slot, out)
         store = [keep.tile([P, U], F32, name="store%d" % b, align_bytes=64) for b in range(2)]
         gate = [keep.tile([P, T], F32, name="gate%d" % b, align_bytes=64) for b in range(2)]
         fresh = keep.tile([P, T], F32, name="fresh", align_bytes=64)
-        warm_out = keep.tile([P, WARM_COLUMNS], F32, name="warm_out")
 
         x_rows = x_words[0].rearrange("p c r -> p (c r)").bitcast(I32)
         scale_rows = x_scales[0].bitcast(I32)
@@ -98,11 +96,10 @@ def tile_picked_widxput_gate_l_kernel(tc, x_words, x_scales, mem, w1, slot, out)
             nc.vector.tensor_tensor(listed(b, first, last), old[b][:, first:last], gate[b][:, first:last], MULT)
 
         nc.sync.dma_start(w_raw[:], w1.rearrange("(p j) c -> p j c", j=PACK))
-        nc.scalar.activation(warm_out[:], w_raw[:, 0, 0:WARM_COLUMNS], SIGMOID)
         nc.sync.dma_start(offsets[:], slot)
-        load_store(0)
         load_scales()
         load_updates(0, QUARTER)
+        load_store(0)
         load_updates(QUARTER, T)
         load_store(1)
 
@@ -110,22 +107,24 @@ def tile_picked_widxput_gate_l_kernel(tc, x_words, x_scales, mem, w1, slot, out)
             group_weights(b)
         for b in range(2):
             quantize_weights(b)
+        for b in range(2):
+            make_gate(b, 0, QUARTER, QUARTERS * b)
 
         nc.vector.tensor_copy(old[0][:, 0:A_GATHER], listed(0, 0, A_GATHER))
         nc.scalar.activation(old[0][:, A_GATHER:T], listed(0, A_GATHER, T), COPY)
-        make_gate(0, 0, QUARTER // 2, 0)
-        make_gate(0, QUARTER // 2, QUARTER, 1)
         for b in range(2):
-            for a in range(1 - b, QUARTERS - 1 + b):
-                make_gate(b, a * QUARTER, (a + 1) * QUARTER, 1 + 3 * b + a)
-        make_gate(0, T - QUARTER, T, 0)
+            for a in range(1, QUARTERS - 1 + b):
+                make_gate(b, a * QUARTER, (a + 1) * QUARTER, QUARTERS * b + a)
+        make_gate(0, T - QUARTER, T, QUARTERS - 1)
         put_product(0, 0, A_VECTOR)
-        for cols in (slice(A_VECTOR, T - QUARTER), slice(T - QUARTER, T)):
+        for cols in (slice(A_CUT, T - QUARTER), slice(T - QUARTER, T)):
             nc.vector.tensor_tensor(fresh[:, cols], old[0][:, cols], gate[0][:, cols], MULT)
+        second = gate[0][:, A_CUT:T]
+        nc.gpsimd.tensor_tensor(second, old[0][:, A_VECTOR:A_CUT], gate[0][:, A_VECTOR:A_CUT], MULT)
         nc.scalar.activation(old[1][:, 0:B_GATHER], listed(1, 0, B_GATHER), COPY)
         nc.vector.tensor_copy(old[1][:, B_GATHER:T], listed(1, B_GATHER, T))
         nc.scalar.activation(listed(0, A_CUT, T), fresh[:, A_CUT:T], COPY)
-        nc.scalar.activation(listed(0, A_VECTOR, A_CUT), fresh[:, A_VECTOR:A_CUT], COPY)
+        nc.scalar.activation(listed(0, A_VECTOR, A_CUT), second, COPY)
         nc.scalar.dma_start(out[0:P, :], store[0][:])
         put_product(1, 0, T)
         for cols in (slice(0, U // 2), slice(U // 2, U)):

@@ -23,10 +23,10 @@ QUADRANT = 32
 SCALE_ROWS = 4
 QUARTERS = 4
 QUARTER = T // QUARTERS
-A_GATHER = 512
-A_VECTOR = QUARTER
-A_CUT = 640
-B_GATHER = 544
+LAST = T - QUARTER
+HALF = T // 2
+MIDDLE = (QUARTER + T) // 2
+SCALAR_GATHER = 544
 
 
 def tile_picked_widxput_gate_l_kernel(tc, x_words, x_scales, mem, w1, slot, out):
@@ -44,8 +44,11 @@ def tile_picked_widxput_gate_l_kernel(tc, x_words, x_scales, mem, w1, slot, out)
         w_codes = [keep.tile([P, P], U32, name="w_codes%d" % b, align_bytes=64) for b in range(2)]
         w_scale = [keep.tile([P, P], U8, name="w_scale%d" % b, align_bytes=64) for b in range(2)]
         store = [keep.tile([P, U], F32, name="store%d" % b, align_bytes=64) for b in range(2)]
-        gate = [keep.tile([P, T], F32, name="gate%d" % b, align_bytes=64) for b in range(2)]
-        fresh = keep.tile([P, T], F32, name="fresh", align_bytes=64)
+        gate = [keep.tile([P, (LAST, T)[b]], F32, name="gate%d" % b, align_bytes=64) for b in range(2)]
+        first_new = keep.tile([P, T - MIDDLE], F32, name="first_new", align_bytes=64)
+        second_new = keep.tile([P, MIDDLE - QUARTER], F32, name="second_new", align_bytes=64)
+        head = MIDDLE - QUARTER - QUARTER
+        last_gate = second_new[:, head:]
 
         x_rows = x_words[0].rearrange("p c r -> p (c r)").bitcast(I32)
         scale_rows = x_scales[0].bitcast(I32)
@@ -58,73 +61,70 @@ def tile_picked_widxput_gate_l_kernel(tc, x_words, x_scales, mem, w1, slot, out)
         def load_updates(first, last):
             nc.sync.dma_start(x_codes[:, first:last].bitcast(I32), x_rows[:, first:last])
 
-        def group_weights(b):
-            nc.vector.tensor_copy(w_grouped[b][:], w_raw[:, :, b * P : (b + 1) * P].rearrange("p j c -> p c j"))
-
-        def quantize_weights(b):
-            nc.vector.quantize_mx(
-                out=w_codes[b][:].bitcast(FP8X4),
-                scales=w_scale[b][:],
-                in_=w_grouped[b][:].rearrange("p c j -> p (c j)"),
-            )
-
-        def make_gate(b, first, last, bank):
-            cols = slice(first, last)
-            acc = psum.tile([P, last - first], F32, name="bank%d" % bank)
+        def make_gate(b, a, target):
+            acc = psum.tile([P, QUARTER], F32, name="bank%d" % (QUARTERS * b + a))
             nc.tensor.matmul_mx(
                 out=acc[:],
                 lhsT=w_codes[b][:].bitcast(FP8X4),
                 lhsT_scale=w_scale[b][:],
-                rhs=x_codes[:, cols].bitcast(FP8X4),
-                rhs_scale=x_scale[SCALE_ROWS * (first // QUARTER) : P, first % QUARTER : first % QUARTER + last - first],
+                rhs=x_codes[:, a * QUARTER : (a + 1) * QUARTER].bitcast(FP8X4),
+                rhs_scale=x_scale[SCALE_ROWS * a : P, :],
                 start=True,
                 stop=True,
             )
-            nc.scalar.activation(gate[b][:, cols], acc[:], SIGMOID)
+            nc.scalar.activation(target, acc[:], SIGMOID)
+
+        def gate_quarter(b, a):
+            return gate[b][:, a * QUARTER : (a + 1) * QUARTER]
 
         def listed(b, first, last):
             return store[b][:].indirect(offsets[:, first // LIST_ROWS : last // LIST_ROWS])
-
-        def load_scales():
-            for q in range(P // QUADRANT):
-                nc.sync.dma_start(
-                    x_scale[QUADRANT * q : QUADRANT * q + QUARTERS * SCALE_ROWS, :].bitcast(I32),
-                    scale_rows[SCALE_ROWS * q : SCALE_ROWS * (q + 1), :].rearrange("r (a c) -> a r c", a=QUARTERS),
-                )
 
         def put_product(b, first, last):
             nc.vector.tensor_tensor(listed(b, first, last), old[b][:, first:last], gate[b][:, first:last], MULT)
 
         nc.sync.dma_start(w_raw[:], w1.rearrange("(p j) c -> p j c", j=PACK))
         nc.sync.dma_start(offsets[:], slot)
-        load_scales()
+        for q in range(P // QUADRANT):
+            nc.sync.dma_start(
+                x_scale[QUADRANT * q : QUADRANT * q + QUARTERS * SCALE_ROWS, :].bitcast(I32),
+                scale_rows[SCALE_ROWS * q : SCALE_ROWS * (q + 1), :].rearrange("r (a c) -> a r c", a=QUARTERS),
+            )
         load_updates(0, QUARTER)
         load_store(0)
         load_updates(QUARTER, T)
         load_store(1)
 
         for b in range(2):
-            group_weights(b)
+            nc.vector.tensor_copy(w_grouped[b][:], w_raw[:, :, b * P : (b + 1) * P].rearrange("p j c -> p c j"))
         for b in range(2):
-            quantize_weights(b)
+            nc.vector.quantize_mx(
+                out=w_codes[b][:].bitcast(FP8X4),
+                scales=w_scale[b][:],
+                in_=w_grouped[b][:].rearrange("p c j -> p (c j)"),
+            )
         for b in range(2):
-            make_gate(b, 0, QUARTER, QUARTERS * b)
+            make_gate(b, 0, gate_quarter(b, 0))
 
-        nc.vector.tensor_copy(old[0][:, 0:A_GATHER], listed(0, 0, A_GATHER))
-        nc.scalar.activation(old[0][:, A_GATHER:T], listed(0, A_GATHER, T), COPY)
+        nc.vector.tensor_copy(old[0][:, 0:HALF], listed(0, 0, HALF))
+        nc.scalar.activation(old[0][:, HALF:T], listed(0, HALF, T), COPY)
         for b in range(2):
             for a in range(1, QUARTERS - 1 + b):
-                make_gate(b, a * QUARTER, (a + 1) * QUARTER, QUARTERS * b + a)
-        make_gate(0, T - QUARTER, T, QUARTERS - 1)
-        put_product(0, 0, A_VECTOR)
-        for cols in (slice(A_CUT, T - QUARTER), slice(T - QUARTER, T)):
-            nc.vector.tensor_tensor(fresh[:, cols], old[0][:, cols], gate[0][:, cols], MULT)
-        second = gate[0][:, A_CUT:T]
-        nc.gpsimd.tensor_tensor(second, old[0][:, A_VECTOR:A_CUT], gate[0][:, A_VECTOR:A_CUT], MULT)
-        nc.scalar.activation(old[1][:, 0:B_GATHER], listed(1, 0, B_GATHER), COPY)
-        nc.vector.tensor_copy(old[1][:, B_GATHER:T], listed(1, B_GATHER, T))
-        nc.scalar.activation(listed(0, A_CUT, T), fresh[:, A_CUT:T], COPY)
-        nc.scalar.activation(listed(0, A_VECTOR, A_CUT), second, COPY)
+                make_gate(b, a, gate_quarter(b, a))
+        make_gate(0, QUARTERS - 1, last_gate)
+
+        put_product(0, 0, QUARTER)
+        cut = QUARTER + head
+        nc.vector.tensor_tensor(second_new[:, 0:head], old[0][:, QUARTER:cut], gate[0][:, QUARTER:cut], MULT)
+        nc.vector.tensor_tensor(first_new[:, 0 : LAST - MIDDLE], old[0][:, MIDDLE:LAST], gate[0][:, MIDDLE:LAST], MULT)
+        nc.vector.tensor_tensor(first_new[:, LAST - MIDDLE :], old[0][:, LAST:T], last_gate, MULT)
+        nc.gpsimd.tensor_tensor(second_new[:, head:], old[0][:, cut:MIDDLE], gate[0][:, cut:MIDDLE], MULT)
+
+        nc.scalar.activation(old[1][:, 0:SCALAR_GATHER], listed(1, 0, SCALAR_GATHER), COPY)
+        nc.vector.tensor_copy(old[1][:, SCALAR_GATHER:T], listed(1, SCALAR_GATHER, T))
+
+        nc.scalar.activation(listed(0, MIDDLE, T), first_new[:], COPY)
+        nc.scalar.activation(listed(0, QUARTER, MIDDLE), second_new[:], COPY)
         nc.scalar.dma_start(out[0:P, :], store[0][:])
         put_product(1, 0, T)
         for cols in (slice(0, U // 2), slice(U // 2, U)):

@@ -24,9 +24,10 @@ SCALE_ROWS = 4
 QUARTERS = 4
 QUARTER = T // QUARTERS
 LAST = T - QUARTER
-HALF = T // 2
+VECTOR_GATHER = 576
 MIDDLE = (QUARTER + T) // 2
-SCALAR_GATHER = 544
+SCALAR_GATHER = 512
+WARM_COLUMNS = 8
 
 
 def tile_picked_widxput_gate_l_kernel(tc, x_words, x_scales, mem, w1, slot, out):
@@ -49,6 +50,7 @@ def tile_picked_widxput_gate_l_kernel(tc, x_words, x_scales, mem, w1, slot, out)
         second_new = keep.tile([P, MIDDLE - QUARTER], F32, name="second_new", align_bytes=64)
         head = MIDDLE - QUARTER - QUARTER
         last_gate = second_new[:, head:]
+        warm_out = keep.tile([P, WARM_COLUMNS], F32, name="warm_out")
 
         x_rows = x_words[0].rearrange("p c r -> p (c r)").bitcast(I32)
         scale_rows = x_scales[0].bitcast(I32)
@@ -61,21 +63,18 @@ def tile_picked_widxput_gate_l_kernel(tc, x_words, x_scales, mem, w1, slot, out)
         def load_updates(first, last):
             nc.sync.dma_start(x_codes[:, first:last].bitcast(I32), x_rows[:, first:last])
 
-        def make_gate(b, a, target):
-            acc = psum.tile([P, QUARTER], F32, name="bank%d" % (QUARTERS * b + a))
+        def make_gate(b, first, last, target, bank):
+            acc = psum.tile([P, last - first], F32, name="bank%d" % bank)
             nc.tensor.matmul_mx(
                 out=acc[:],
                 lhsT=w_codes[b][:].bitcast(FP8X4),
                 lhsT_scale=w_scale[b][:],
-                rhs=x_codes[:, a * QUARTER : (a + 1) * QUARTER].bitcast(FP8X4),
-                rhs_scale=x_scale[SCALE_ROWS * a : P, :],
+                rhs=x_codes[:, first:last].bitcast(FP8X4),
+                rhs_scale=x_scale[SCALE_ROWS * (first // QUARTER) : P, first % QUARTER : first % QUARTER + last - first],
                 start=True,
                 stop=True,
             )
             nc.scalar.activation(target, acc[:], SIGMOID)
-
-        def gate_quarter(b, a):
-            return gate[b][:, a * QUARTER : (a + 1) * QUARTER]
 
         def listed(b, first, last):
             return store[b][:].indirect(offsets[:, first // LIST_ROWS : last // LIST_ROWS])
@@ -84,14 +83,15 @@ def tile_picked_widxput_gate_l_kernel(tc, x_words, x_scales, mem, w1, slot, out)
             nc.vector.tensor_tensor(listed(b, first, last), old[b][:, first:last], gate[b][:, first:last], MULT)
 
         nc.sync.dma_start(w_raw[:], w1.rearrange("(p j) c -> p j c", j=PACK))
+        nc.scalar.activation(warm_out[:], w_raw[:, 0, 0:WARM_COLUMNS], SIGMOID)
         nc.sync.dma_start(offsets[:], slot)
+        load_store(0)
         for q in range(P // QUADRANT):
             nc.sync.dma_start(
                 x_scale[QUADRANT * q : QUADRANT * q + QUARTERS * SCALE_ROWS, :].bitcast(I32),
                 scale_rows[SCALE_ROWS * q : SCALE_ROWS * (q + 1), :].rearrange("r (a c) -> a r c", a=QUARTERS),
             )
         load_updates(0, QUARTER)
-        load_store(0)
         load_updates(QUARTER, T)
         load_store(1)
 
@@ -103,15 +103,15 @@ def tile_picked_widxput_gate_l_kernel(tc, x_words, x_scales, mem, w1, slot, out)
                 scales=w_scale[b][:],
                 in_=w_grouped[b][:].rearrange("p c j -> p (c j)"),
             )
-        for b in range(2):
-            make_gate(b, 0, gate_quarter(b, 0))
 
-        nc.vector.tensor_copy(old[0][:, 0:HALF], listed(0, 0, HALF))
-        nc.scalar.activation(old[0][:, HALF:T], listed(0, HALF, T), COPY)
-        for b in range(2):
-            for a in range(1, QUARTERS - 1 + b):
-                make_gate(b, a, gate_quarter(b, a))
-        make_gate(0, QUARTERS - 1, last_gate)
+        nc.vector.tensor_copy(old[0][:, 0:VECTOR_GATHER], listed(0, 0, VECTOR_GATHER))
+        nc.scalar.activation(old[0][:, VECTOR_GATHER:T], listed(0, VECTOR_GATHER, T), COPY)
+        pieces = [(0, 0, QUARTER // 2), (0, QUARTER // 2, QUARTER)]
+        pieces.extend((0, first, first + QUARTER) for first in range(QUARTER, LAST, QUARTER))
+        pieces.extend((1, first, first + QUARTER) for first in range(0, T, QUARTER))
+        for bank, (b, first, last) in enumerate(pieces):
+            make_gate(b, first, last, gate[b][:, first:last], bank)
+        make_gate(0, LAST, T, last_gate, 0)
 
         put_product(0, 0, QUARTER)
         cut = QUARTER + head

@@ -23,10 +23,13 @@ QUADRANT = 32
 SCALE_ROWS = 4
 QUARTERS = 4
 QUARTER = T // QUARTERS
-LAST = T - QUARTER
-VECTOR_GATHER = 576
-MIDDLE = (QUARTER + T) // 2
-SCALAR_GATHER = 512
+BANKS = 8
+PIECE = QUARTER // 2
+OWN = 384
+SECOND = OWN + QUARTER
+LATE = PIECE
+STORE_CUT = 3 * U // 4
+SCALAR_GATHER = (384, 448)
 WARM_COLUMNS = 8
 
 
@@ -45,11 +48,9 @@ def tile_picked_widxput_gate_l_kernel(tc, x_words, x_scales, mem, w1, slot, out)
         w_codes = [keep.tile([P, P], U32, name="w_codes%d" % b, align_bytes=64) for b in range(2)]
         w_scale = [keep.tile([P, P], U8, name="w_scale%d" % b, align_bytes=64) for b in range(2)]
         store = [keep.tile([P, U], F32, name="store%d" % b, align_bytes=64) for b in range(2)]
-        gate = [keep.tile([P, (LAST, T)[b]], F32, name="gate%d" % b, align_bytes=64) for b in range(2)]
-        first_new = keep.tile([P, T - MIDDLE], F32, name="first_new", align_bytes=64)
-        second_new = keep.tile([P, MIDDLE - QUARTER], F32, name="second_new", align_bytes=64)
-        head = MIDDLE - QUARTER - QUARTER
-        last_gate = second_new[:, head:]
+        gate = [keep.tile([P, T], F32, name="gate%d" % b, align_bytes=64) for b in range(2)]
+        first_new = keep.tile([P, OWN], F32, name="first_new", align_bytes=64)
+        second_new = old[0][:, 0 : T - SECOND]
         warm_out = keep.tile([P, WARM_COLUMNS], F32, name="warm_out")
 
         x_rows = x_words[0].rearrange("p c r -> p (c r)").bitcast(I32)
@@ -57,13 +58,13 @@ def tile_picked_widxput_gate_l_kernel(tc, x_words, x_scales, mem, w1, slot, out)
 
         nc.vector.memset(x_scale[:].bitcast(I32), 0)
 
-        def load_store(b):
-            nc.sync.dma_start(store[b][:], mem[b * P : (b + 1) * P, :])
+        def load_store(b, first, last):
+            nc.sync.dma_start(store[b][:, first:last], mem[b * P : (b + 1) * P, first:last])
 
         def load_updates(first, last):
             nc.sync.dma_start(x_codes[:, first:last].bitcast(I32), x_rows[:, first:last])
 
-        def make_gate(b, first, last, target, bank):
+        def make_gate(b, first, last, bank):
             acc = psum.tile([P, last - first], F32, name="bank%d" % bank)
             nc.tensor.matmul_mx(
                 out=acc[:],
@@ -74,26 +75,33 @@ def tile_picked_widxput_gate_l_kernel(tc, x_words, x_scales, mem, w1, slot, out)
                 start=True,
                 stop=True,
             )
-            nc.scalar.activation(target, acc[:], SIGMOID)
+            nc.scalar.activation(gate[b][:, first:last], acc[:], SIGMOID)
 
         def listed(b, first, last):
             return store[b][:].indirect(offsets[:, first // LIST_ROWS : last // LIST_ROWS])
 
-        def put_product(b, first, last):
-            nc.vector.tensor_tensor(listed(b, first, last), old[b][:, first:last], gate[b][:, first:last], MULT)
+        def gather(b):
+            cut = SCALAR_GATHER[b]
+            nc.scalar.activation(old[b][:, 0:cut], listed(b, 0, cut), COPY)
+            nc.vector.tensor_copy(old[b][:, cut:T], listed(b, cut, T))
+
+        def multiply(engine, target, b, first, last):
+            engine.tensor_tensor(target, old[b][:, first:last], gate[b][:, first:last], MULT)
 
         nc.sync.dma_start(w_raw[:], w1.rearrange("(p j) c -> p j c", j=PACK))
         nc.scalar.activation(warm_out[:], w_raw[:, 0, 0:WARM_COLUMNS], SIGMOID)
         nc.sync.dma_start(offsets[:], slot)
-        load_store(0)
+        load_store(0, 0, U)
         for q in range(P // QUADRANT):
             nc.sync.dma_start(
                 x_scale[QUADRANT * q : QUADRANT * q + QUARTERS * SCALE_ROWS, :].bitcast(I32),
                 scale_rows[SCALE_ROWS * q : SCALE_ROWS * (q + 1), :].rearrange("r (a c) -> a r c", a=QUARTERS),
             )
-        load_updates(0, QUARTER)
-        load_updates(QUARTER, T)
-        load_store(1)
+        load_updates(LATE, SECOND)
+        load_updates(SECOND, T)
+        load_store(1, 0, STORE_CUT)
+        load_updates(0, LATE)
+        load_store(1, STORE_CUT, U)
 
         for b in range(2):
             nc.vector.tensor_copy(w_grouped[b][:], w_raw[:, :, b * P : (b + 1) * P].rearrange("p j c -> p c j"))
@@ -104,28 +112,23 @@ def tile_picked_widxput_gate_l_kernel(tc, x_words, x_scales, mem, w1, slot, out)
                 in_=w_grouped[b][:].rearrange("p c j -> p (c j)"),
             )
 
-        nc.vector.tensor_copy(old[0][:, 0:VECTOR_GATHER], listed(0, 0, VECTOR_GATHER))
-        nc.scalar.activation(old[0][:, VECTOR_GATHER:T], listed(0, VECTOR_GATHER, T), COPY)
-        pieces = [(0, 0, QUARTER // 2), (0, QUARTER // 2, QUARTER)]
-        pieces.extend((0, first, first + QUARTER) for first in range(QUARTER, LAST, QUARTER))
-        pieces.extend((1, first, first + QUARTER) for first in range(0, T, QUARTER))
-        for bank, (b, first, last) in enumerate(pieces):
-            make_gate(b, first, last, gate[b][:, first:last], bank)
-        make_gate(0, LAST, T, last_gate, 0)
+        gather(0)
+        pieces = [(0, first, first + PIECE) for first in range(LATE, SECOND, PIECE)]
+        pieces.extend([(1, LATE, QUARTER), (1, QUARTER, 2 * QUARTER), (0, SECOND, 3 * QUARTER), (0, 3 * QUARTER, T)])
+        pieces.extend([(1, 2 * QUARTER, 3 * QUARTER), (1, 3 * QUARTER, T), (1, 0, LATE), (0, 0, LATE)])
+        for piece, (b, first, last) in enumerate(pieces):
+            make_gate(b, first, last, piece % BANKS)
 
-        put_product(0, 0, QUARTER)
-        cut = QUARTER + head
-        nc.vector.tensor_tensor(second_new[:, 0:head], old[0][:, QUARTER:cut], gate[0][:, QUARTER:cut], MULT)
-        nc.vector.tensor_tensor(first_new[:, 0 : LAST - MIDDLE], old[0][:, MIDDLE:LAST], gate[0][:, MIDDLE:LAST], MULT)
-        nc.vector.tensor_tensor(first_new[:, LAST - MIDDLE :], old[0][:, LAST:T], last_gate, MULT)
-        nc.gpsimd.tensor_tensor(second_new[:, head:], old[0][:, cut:MIDDLE], gate[0][:, cut:MIDDLE], MULT)
+        multiply(nc.vector, first_new[:, LATE:OWN], 0, LATE, OWN)
+        multiply(nc.vector, listed(0, OWN, SECOND), 0, OWN, SECOND)
+        multiply(nc.gpsimd, first_new[:, 0:LATE], 0, 0, LATE)
 
-        nc.scalar.activation(old[1][:, 0:SCALAR_GATHER], listed(1, 0, SCALAR_GATHER), COPY)
-        nc.vector.tensor_copy(old[1][:, SCALAR_GATHER:T], listed(1, SCALAR_GATHER, T))
+        gather(1)
+        multiply(nc.vector, second_new, 0, SECOND, T)
 
-        nc.scalar.activation(listed(0, MIDDLE, T), first_new[:], COPY)
-        nc.scalar.activation(listed(0, QUARTER, MIDDLE), second_new[:], COPY)
+        nc.scalar.activation(listed(0, 0, OWN), first_new[:], COPY)
+        nc.scalar.activation(listed(0, SECOND, T), second_new, COPY)
         nc.scalar.dma_start(out[0:P, :], store[0][:])
-        put_product(1, 0, T)
+        multiply(nc.vector, listed(1, 0, T), 1, 0, T)
         for cols in (slice(0, U // 2), slice(U // 2, U)):
             nc.sync.dma_start(out[P : 2 * P, cols], store[1][:, cols])

@@ -25,11 +25,11 @@ QUARTERS = 4
 QUARTER = T // QUARTERS
 BANKS = 8
 PIECE = QUARTER // 2
-OWN = 384
-SECOND = OWN + QUARTER
+OWN = 320
+SECOND = 640
 LATE = PIECE
 STORE_CUT = 3 * U // 4
-SCALAR_GATHER = (384, 448)
+SCALAR_GATHER = (384, 512)
 WARM_COLUMNS = 8
 
 

@@ -25,11 +25,11 @@ QUARTERS = 4
 QUARTER = T // QUARTERS
 BANKS = 8
 PIECE = QUARTER // 2
-OWN = 320
+OWN = 288
 SECOND = 640
-LATE = PIECE
-STORE_CUT = 3 * U // 4
-SCALAR_GATHER = (384, 512)
+LATE = QUARTER
+STORE_CUT = 5 * U // 8
+SCALAR_GATHER = (448, 544)
 WARM_COLUMNS = 8
 
 
@@ -114,7 +114,7 @@ def tile_picked_widxput_gate_l_kernel(tc, x_words, x_scales, mem, w1, slot, out)
 
         gather(0)
         pieces = [(0, first, first + PIECE) for first in range(LATE, SECOND, PIECE)]
-        pieces.extend([(1, LATE, QUARTER), (1, QUARTER, 2 * QUARTER), (0, SECOND, 3 * QUARTER), (0, 3 * QUARTER, T)])
+        pieces.extend([(1, QUARTER, 2 * QUARTER), (0, SECOND, 3 * QUARTER), (0, 3 * QUARTER, T)])
         pieces.extend([(1, 2 * QUARTER, 3 * QUARTER), (1, 3 * QUARTER, T), (1, 0, LATE), (0, 0, LATE)])
         for piece, (b, first, last) in enumerate(pieces):
             make_gate(b, first, last, piece % BANKS)

@@ -29,7 +29,7 @@ OWN = 288
 SECOND = 640
 LATE = QUARTER
 STORE_CUT = 5 * U // 8
-SCALAR_GATHER = (448, 544)
+SCALAR_GATHER = (448, 576)
 WARM_COLUMNS = 8
 
 
@@ -115,7 +115,7 @@ def tile_picked_widxput_gate_l_kernel(tc, x_words, x_scales, mem, w1, slot, out)
         gather(0)
         pieces = [(0, first, first + PIECE) for first in range(LATE, SECOND, PIECE)]
         pieces.extend([(1, QUARTER, 2 * QUARTER), (0, SECOND, 3 * QUARTER), (0, 3 * QUARTER, T)])
-        pieces.extend([(1, 2 * QUARTER, 3 * QUARTER), (1, 3 * QUARTER, T), (1, 0, LATE), (0, 0, LATE)])
+        pieces.extend([(1, 2 * QUARTER, 3 * QUARTER), (1, 3 * QUARTER, T), (0, 0, LATE), (1, 0, LATE)])
         for piece, (b, first, last) in enumerate(pieces):
             make_gate(b, first, last, piece % BANKS)
 
@@ -128,7 +128,7 @@ def tile_picked_widxput_gate_l_kernel(tc, x_words, x_scales, mem, w1, slot, out)
 
         nc.scalar.activation(listed(0, 0, OWN), first_new[:], COPY)
         nc.scalar.activation(listed(0, SECOND, T), second_new, COPY)
-        nc.scalar.dma_start(out[0:P, :], store[0][:])
+        nc.sync.dma_start(out[0:P, :], store[0][:])
         multiply(nc.vector, listed(1, 0, T), 1, 0, T)
         for cols in (slice(0, U // 2), slice(U // 2, U)):
             nc.sync.dma_start(out[P : 2 * P, cols], store[1][:, cols])

@@ -28,7 +28,7 @@ PIECE = QUARTER // 2
 OWN = 288
 SECOND = 640
 LATE = QUARTER
-STORE_CUT = 5 * U // 8
+STORE_CUT = 9 * U // 16
 SCALAR_GATHER = (448, 576)
 WARM_COLUMNS = 8
 

@@ -25,10 +25,10 @@ QUARTERS = 4
 QUARTER = T // QUARTERS
 BANKS = 8
 PIECE = QUARTER // 2
-OWN = 288
-SECOND = 640
 LATE = QUARTER
-STORE_CUT = 9 * U // 16
+SECOND = LATE + 3 * PIECE
+OWN = 288
+STORE_CUT = U // 2
 SCALAR_GATHER = (448, 576)
 WARM_COLUMNS = 8
 
@@ -115,7 +115,7 @@ def tile_picked_widxput_gate_l_kernel(tc, x_words, x_scales, mem, w1, slot, out)
         gather(0)
         pieces = [(0, first, first + PIECE) for first in range(LATE, SECOND, PIECE)]
         pieces.extend([(1, QUARTER, 2 * QUARTER), (0, SECOND, 3 * QUARTER), (0, 3 * QUARTER, T)])
-        pieces.extend([(1, 2 * QUARTER, 3 * QUARTER), (1, 3 * QUARTER, T), (0, 0, LATE), (1, 0, LATE)])
+        pieces.extend([(1, 2 * QUARTER, 3 * QUARTER), (1, 3 * QUARTER, T), (1, 0, LATE), (0, 0, LATE)])
         for piece, (b, first, last) in enumerate(pieces):
             make_gate(b, first, last, piece % BANKS)
 

@@ -21,15 +21,13 @@ PACK = 4
 LIST_ROWS = 16
 QUADRANT = 32
 SCALE_ROWS = 4
-QUARTERS = 4
-QUARTER = T // QUARTERS
 BANKS = 8
-PIECE = QUARTER // 2
-LATE = QUARTER
-SECOND = LATE + 3 * PIECE
-OWN = 288
-STORE_CUT = U // 2
+PIECE = 128
+EARLY = 3 * PIECE
+FIRST = 320
+SECOND = 640
 SCALAR_GATHER = (448, 576)
+FUSED = 64
 WARM_COLUMNS = 8
 
 
@@ -40,7 +38,8 @@ def tile_picked_widxput_gate_l_kernel(tc, x_words, x_scales, mem, w1, slot, out)
         psum = ctx.enter_context(tc.psum_pool(name="psum", bufs=1))
 
         offsets = keep.tile([P, T // LIST_ROWS], U16, name="offsets")
-        x_scale = keep.tile([P, QUARTER], U8, name="x_scale", align_bytes=64)
+        early_scale = keep.tile([P, EARLY], U8, name="early_scale", align_bytes=64)
+        late_scale = keep.tile([P, T - EARLY], U8, name="late_scale", align_bytes=64)
         x_codes = keep.tile([P, T], U32, name="x_codes", align_bytes=64)
         old = [keep.tile([P, T], F32, name="old%d" % b, align_bytes=64) for b in range(2)]
         w_raw = keep.tile([P, PACK, N], F32, name="w_raw", align_bytes=64)
@@ -49,41 +48,55 @@ def tile_picked_widxput_gate_l_kernel(tc, x_words, x_scales, mem, w1, slot, out)
         w_scale = [keep.tile([P, P], U8, name="w_scale%d" % b, align_bytes=64) for b in range(2)]
         store = [keep.tile([P, U], F32, name="store%d" % b, align_bytes=64) for b in range(2)]
         gate = [keep.tile([P, T], F32, name="gate%d" % b, align_bytes=64) for b in range(2)]
-        first_new = keep.tile([P, OWN], F32, name="first_new", align_bytes=64)
-        second_new = old[0][:, 0 : T - SECOND]
+        first_new = keep.tile([P, SECOND - FIRST], F32, name="first_new", align_bytes=64)
+        second_new = old[0][:, SECOND - (T - SECOND) : SECOND]
+        fused_first = SCALAR_GATHER[1]
+        fused_last = fused_first + FUSED
+        fused_gate = first_new[:, EARLY - FIRST : EARLY - FIRST + FUSED]
         warm_out = keep.tile([P, WARM_COLUMNS], F32, name="warm_out")
 
         x_rows = x_words[0].rearrange("p c r -> p (c r)").bitcast(I32)
         scale_rows = x_scales[0].bitcast(I32)
 
-        nc.vector.memset(x_scale[:].bitcast(I32), 0)
+        nc.vector.memset(early_scale[:].bitcast(I32), 0)
+        nc.vector.memset(late_scale[:].bitcast(I32), 0)
+        nc.vector.memset(gate[1][:, fused_first:fused_last], 1.0)
 
-        def load_store(b, first, last):
-            nc.sync.dma_start(store[b][:, first:last], mem[b * P : (b + 1) * P, first:last])
+        def load_scales(tile, first, last):
+            for r in range(SCALE_ROWS):
+                nc.sync.dma_start(
+                    tile[r:P:QUADRANT, :].bitcast(I32),
+                    scale_rows[r : P // 8 : SCALE_ROWS, first // PACK : last // PACK],
+                )
 
         def load_updates(first, last):
             nc.sync.dma_start(x_codes[:, first:last].bitcast(I32), x_rows[:, first:last])
 
         def make_gate(b, first, last, bank):
+            scale, start = (early_scale, 0) if first < EARLY else (late_scale, EARLY)
             acc = psum.tile([P, last - first], F32, name="bank%d" % bank)
             nc.tensor.matmul_mx(
                 out=acc[:],
                 lhsT=w_codes[b][:].bitcast(FP8X4),
                 lhsT_scale=w_scale[b][:],
                 rhs=x_codes[:, first:last].bitcast(FP8X4),
-                rhs_scale=x_scale[SCALE_ROWS * (first // QUARTER) : P, first % QUARTER : first % QUARTER + last - first],
+                rhs_scale=scale[:, first - start : last - start],
                 start=True,
                 stop=True,
             )
-            nc.scalar.activation(gate[b][:, first:last], acc[:], SIGMOID)
+            if b == 1 and last == fused_last:
+                nc.scalar.activation(gate[b][:, first:fused_first], acc[:, 0 : fused_first - first], SIGMOID)
+                nc.scalar.activation(fused_gate, acc[:, fused_first - first : last - first], SIGMOID)
+            else:
+                nc.scalar.activation(gate[b][:, first:last], acc[:], SIGMOID)
 
-        def listed(b, first, last):
-            return store[b][:].indirect(offsets[:, first // LIST_ROWS : last // LIST_ROWS])
+        def listed(tile, first, last):
+            return tile[:].indirect(offsets[:, first // LIST_ROWS : last // LIST_ROWS])
 
-        def gather(b):
+        def gather(b, first):
             cut = SCALAR_GATHER[b]
-            nc.scalar.activation(old[b][:, 0:cut], listed(b, 0, cut), COPY)
-            nc.vector.tensor_copy(old[b][:, cut:T], listed(b, cut, T))
+            nc.scalar.activation(old[b][:, 0:cut], listed(store[b], 0, cut), COPY)
+            nc.vector.tensor_copy(old[b][:, first:T], listed(store[b], first, T))
 
         def multiply(engine, target, b, first, last):
             engine.tensor_tensor(target, old[b][:, first:last], gate[b][:, first:last], MULT)
@@ -91,17 +104,12 @@ def tile_picked_widxput_gate_l_kernel(tc, x_words, x_scales, mem, w1, slot, out)
         nc.sync.dma_start(w_raw[:], w1.rearrange("(p j) c -> p j c", j=PACK))
         nc.scalar.activation(warm_out[:], w_raw[:, 0, 0:WARM_COLUMNS], SIGMOID)
         nc.sync.dma_start(offsets[:], slot)
-        load_store(0, 0, U)
-        for q in range(P // QUADRANT):
-            nc.sync.dma_start(
-                x_scale[QUADRANT * q : QUADRANT * q + QUARTERS * SCALE_ROWS, :].bitcast(I32),
-                scale_rows[SCALE_ROWS * q : SCALE_ROWS * (q + 1), :].rearrange("r (a c) -> a r c", a=QUARTERS),
-            )
-        load_updates(LATE, SECOND)
-        load_updates(SECOND, T)
-        load_store(1, 0, STORE_CUT)
-        load_updates(0, LATE)
-        load_store(1, STORE_CUT, U)
+        load_scales(early_scale, 0, EARLY)
+        nc.sync.dma_start(store[0][:], mem[0:P, :])
+        load_updates(0, EARLY)
+        load_scales(late_scale, EARLY, T)
+        load_updates(EARLY, T)
+        nc.sync.dma_start(store[1][:], mem[P : 2 * P, :])
 
         for b in range(2):
             nc.vector.tensor_copy(w_grouped[b][:], w_raw[:, :, b * P : (b + 1) * P].rearrange("p j c -> p c j"))
@@ -112,23 +120,24 @@ def tile_picked_widxput_gate_l_kernel(tc, x_words, x_scales, mem, w1, slot, out)
                 in_=w_grouped[b][:].rearrange("p c j -> p (c j)"),
             )
 
-        gather(0)
-        pieces = [(0, first, first + PIECE) for first in range(LATE, SECOND, PIECE)]
-        pieces.extend([(1, QUARTER, 2 * QUARTER), (0, SECOND, 3 * QUARTER), (0, 3 * QUARTER, T)])
-        pieces.extend([(1, 2 * QUARTER, 3 * QUARTER), (1, 3 * QUARTER, T), (1, 0, LATE), (0, 0, LATE)])
+        gather(0, SCALAR_GATHER[0])
+        pieces = [(0, first, first + PIECE) for first in reversed(range(0, EARLY, PIECE))]
+        pieces.extend([(1, 0, 2 * PIECE), (1, 2 * PIECE, EARLY)])
+        for b in range(2):
+            pieces.extend([(b, EARLY, SECOND), (b, SECOND, SECOND + 2 * PIECE), (b, SECOND + 2 * PIECE, T)])
         for piece, (b, first, last) in enumerate(pieces):
             make_gate(b, first, last, piece % BANKS)
 
-        multiply(nc.vector, first_new[:, LATE:OWN], 0, LATE, OWN)
-        multiply(nc.vector, listed(0, OWN, SECOND), 0, OWN, SECOND)
-        multiply(nc.gpsimd, first_new[:, 0:LATE], 0, 0, LATE)
+        multiply(nc.vector, first_new[:, 0 : EARLY - FIRST], 0, FIRST, EARLY)
+        multiply(nc.vector, listed(store[0], 0, FIRST), 0, 0, FIRST)
 
-        gather(1)
+        nc.vector.tensor_tensor(old[1][:, fused_first:fused_last], listed(store[1], fused_first, fused_last), fused_gate, MULT)
+        multiply(nc.gpsimd, first_new[:, EARLY - FIRST : SECOND - FIRST], 0, EARLY, SECOND)
+        gather(1, fused_last)
         multiply(nc.vector, second_new, 0, SECOND, T)
 
-        nc.scalar.activation(listed(0, 0, OWN), first_new[:], COPY)
-        nc.scalar.activation(listed(0, SECOND, T), second_new, COPY)
+        nc.scalar.activation(listed(store[0], FIRST, SECOND), first_new[:], COPY)
+        nc.scalar.activation(listed(store[0], SECOND, T), second_new, COPY)
         nc.sync.dma_start(out[0:P, :], store[0][:])
-        multiply(nc.vector, listed(1, 0, T), 1, 0, T)
-        for cols in (slice(0, U // 2), slice(U // 2, U)):
-            nc.sync.dma_start(out[P : 2 * P, cols], store[1][:, cols])
+        multiply(nc.vector, listed(store[1], 0, T), 1, 0, T)
+        nc.sync.dma_start(out[P : 2 * P, :], store[1][:])

@@ -24,10 +24,11 @@ SCALE_ROWS = 4
 BANKS = 8
 PIECE = 128
 EARLY = 3 * PIECE
-FIRST = 320
+FIRST = 288
 SECOND = 640
-SCALAR_GATHER = (448, 576)
+SCALAR_GATHER = (448, 480)
 FUSED = 64
+HELD = 64
 WARM_COLUMNS = 8
 
 
@@ -41,18 +42,20 @@ def tile_picked_widxput_gate_l_kernel(tc, x_words, x_scales, mem, w1, slot, out)
         early_scale = keep.tile([P, EARLY], U8, name="early_scale", align_bytes=64)
         late_scale = keep.tile([P, T - EARLY], U8, name="late_scale", align_bytes=64)
         x_codes = keep.tile([P, T], U32, name="x_codes", align_bytes=64)
-        old = [keep.tile([P, T], F32, name="old%d" % b, align_bytes=64) for b in range(2)]
+        old_first = keep.tile([P, T], F32, name="old_first", align_bytes=64)
+        shared = keep.tile([P, SECOND - FIRST + T], F32, name="shared", align_bytes=64)
+        old = [old_first[:], shared[:, SECOND - FIRST :]]
         w_raw = keep.tile([P, PACK, N], F32, name="w_raw", align_bytes=64)
         w_grouped = [keep.tile([P, P, PACK], BF16, name="w_grouped%d" % b, align_bytes=64) for b in range(2)]
         w_codes = [keep.tile([P, P], U32, name="w_codes%d" % b, align_bytes=64) for b in range(2)]
         w_scale = [keep.tile([P, P], U8, name="w_scale%d" % b, align_bytes=64) for b in range(2)]
         store = [keep.tile([P, U], F32, name="store%d" % b, align_bytes=64) for b in range(2)]
         gate = [keep.tile([P, T], F32, name="gate%d" % b, align_bytes=64) for b in range(2)]
-        first_new = keep.tile([P, SECOND - FIRST], F32, name="first_new", align_bytes=64)
+        first_new = shared[:, 0 : SECOND - FIRST]
         second_new = old[0][:, SECOND - (T - SECOND) : SECOND]
-        fused_first = SCALAR_GATHER[1]
-        fused_last = fused_first + FUSED
-        fused_gate = first_new[:, EARLY - FIRST : EARLY - FIRST + FUSED]
+        fused_gate = shared[:, SECOND - FIRST - FUSED // 2 : SECOND - FIRST + FUSED // 2]
+        fused_last = EARLY
+        fused_first = fused_last - FUSED
         warm_out = keep.tile([P, WARM_COLUMNS], F32, name="warm_out")
 
         x_rows = x_words[0].rearrange("p c r -> p (c r)").bitcast(I32)
@@ -93,10 +96,14 @@ def tile_picked_widxput_gate_l_kernel(tc, x_words, x_scales, mem, w1, slot, out)
         def listed(tile, first, last):
             return tile[:].indirect(offsets[:, first // LIST_ROWS : last // LIST_ROWS])
 
-        def gather(b, first):
-            cut = SCALAR_GATHER[b]
-            nc.scalar.activation(old[b][:, 0:cut], listed(store[b], 0, cut), COPY)
-            nc.vector.tensor_copy(old[b][:, first:T], listed(store[b], first, T))
+        def scalar_gather(b, first, last):
+            nc.scalar.activation(old[b][:, first:last], listed(store[b], first, last), COPY)
+
+        def vector_gather(b, first, last):
+            nc.vector.tensor_copy(old[b][:, first:last], listed(store[b], first, last))
+
+        def products(first, last):
+            multiply(nc.vector, first_new[:, first - FIRST : last - FIRST], 0, first, last)
 
         def multiply(engine, target, b, first, last):
             engine.tensor_tensor(target, old[b][:, first:last], gate[b][:, first:last], MULT)
@@ -120,7 +127,8 @@ def tile_picked_widxput_gate_l_kernel(tc, x_words, x_scales, mem, w1, slot, out)
                 in_=w_grouped[b][:].rearrange("p c j -> p (c j)"),
             )
 
-        gather(0, SCALAR_GATHER[0])
+        scalar_gather(0, 0, SCALAR_GATHER[0])
+        vector_gather(0, SCALAR_GATHER[0], T)
         pieces = [(0, first, first + PIECE) for first in reversed(range(0, EARLY, PIECE))]
         pieces.extend([(1, 0, 2 * PIECE), (1, 2 * PIECE, EARLY)])
         for b in range(2):
@@ -128,15 +136,18 @@ def tile_picked_widxput_gate_l_kernel(tc, x_words, x_scales, mem, w1, slot, out)
         for piece, (b, first, last) in enumerate(pieces):
             make_gate(b, first, last, piece % BANKS)
 
-        multiply(nc.vector, first_new[:, 0 : EARLY - FIRST], 0, FIRST, EARLY)
+        products(FIRST, EARLY)
         multiply(nc.vector, listed(store[0], 0, FIRST), 0, 0, FIRST)
+        products(EARLY, SECOND - HELD)
 
+        scalar_gather(1, T - SCALAR_GATHER[1], T)
         nc.vector.tensor_tensor(old[1][:, fused_first:fused_last], listed(store[1], fused_first, fused_last), fused_gate, MULT)
-        multiply(nc.gpsimd, first_new[:, EARLY - FIRST : SECOND - FIRST], 0, EARLY, SECOND)
-        gather(1, fused_last)
+        vector_gather(1, fused_last, T - SCALAR_GATHER[1])
+        products(SECOND - HELD, SECOND)
+        vector_gather(1, 0, fused_first)
         multiply(nc.vector, second_new, 0, SECOND, T)
 
-        nc.scalar.activation(listed(store[0], FIRST, SECOND), first_new[:], COPY)
+        nc.scalar.activation(listed(store[0], FIRST, SECOND), first_new, COPY)
         nc.scalar.activation(listed(store[0], SECOND, T), second_new, COPY)
         nc.sync.dma_start(out[0:P, :], store[0][:])
         multiply(nc.vector, listed(store[1], 0, T), 1, 0, T)

@@ -23,12 +23,12 @@ QUADRANT = 32
 SCALE_ROWS = 4
 BANKS = 8
 PIECE = 128
-EARLY = 3 * PIECE
-FIRST = 288
-SECOND = 640
-SCALAR_GATHER = (448, 480)
-FUSED = 64
-HELD = 64
+LATE = T - 3 * PIECE
+VECTOR_FIRST = 704
+SPLIT = 384
+SCALAR_GATHER = (448, 576)
+LEAD = 64
+DONE = 8
 WARM_COLUMNS = 8
 
 
@@ -39,23 +39,20 @@ def tile_picked_widxput_gate_l_kernel(tc, x_words, x_scales, mem, w1, slot, out)
         psum = ctx.enter_context(tc.psum_pool(name="psum", bufs=1))
 
         offsets = keep.tile([P, T // LIST_ROWS], U16, name="offsets")
-        early_scale = keep.tile([P, EARLY], U8, name="early_scale", align_bytes=64)
-        late_scale = keep.tile([P, T - EARLY], U8, name="late_scale", align_bytes=64)
+        early_scale = keep.tile([P, T - LATE], U8, name="early_scale", align_bytes=64)
+        late_scale = keep.tile([P, LATE], U8, name="late_scale", align_bytes=64)
         x_codes = keep.tile([P, T], U32, name="x_codes", align_bytes=64)
-        old_first = keep.tile([P, T], F32, name="old_first", align_bytes=64)
-        shared = keep.tile([P, SECOND - FIRST + T], F32, name="shared", align_bytes=64)
-        old = [old_first[:], shared[:, SECOND - FIRST :]]
         w_raw = keep.tile([P, PACK, N], F32, name="w_raw", align_bytes=64)
         w_grouped = [keep.tile([P, P, PACK], BF16, name="w_grouped%d" % b, align_bytes=64) for b in range(2)]
         w_codes = [keep.tile([P, P], U32, name="w_codes%d" % b, align_bytes=64) for b in range(2)]
         w_scale = [keep.tile([P, P], U8, name="w_scale%d" % b, align_bytes=64) for b in range(2)]
         store = [keep.tile([P, U], F32, name="store%d" % b, align_bytes=64) for b in range(2)]
-        gate = [keep.tile([P, T], F32, name="gate%d" % b, align_bytes=64) for b in range(2)]
-        first_new = shared[:, 0 : SECOND - FIRST]
-        second_new = old[0][:, SECOND - (T - SECOND) : SECOND]
-        fused_gate = shared[:, SECOND - FIRST - FUSED // 2 : SECOND - FIRST + FUSED // 2]
-        fused_last = EARLY
-        fused_first = fused_last - FUSED
+        values = keep.tile([P, 2 * T - SPLIT], F32, name="values", align_bytes=64)
+        low_values = keep.tile([P, SPLIT], F32, name="low_values", align_bytes=64)
+        second_gate = keep.tile([P, T], F32, name="second_gate", align_bytes=64)
+        high_gate = keep.tile([P, DONE + T - SPLIT], F32, name="high_gate", align_bytes=64)
+        low_gate = keep.tile([P, SPLIT], F32, name="low_gate", align_bytes=64)
+        second_new = high_gate[:, DONE : DONE + SPLIT]
         warm_out = keep.tile([P, WARM_COLUMNS], F32, name="warm_out")
 
         x_rows = x_words[0].rearrange("p c r -> p (c r)").bitcast(I32)
@@ -63,7 +60,21 @@ def tile_picked_widxput_gate_l_kernel(tc, x_words, x_scales, mem, w1, slot, out)
 
         nc.vector.memset(early_scale[:].bitcast(I32), 0)
         nc.vector.memset(late_scale[:].bitcast(I32), 0)
-        nc.vector.memset(gate[1][:, fused_first:fused_last], 1.0)
+        nc.vector.memset(second_gate[:, T - DONE : T], 1.0)
+
+        def old(b, first, last):
+            if b == 1:
+                return values[:, first:last]
+            if first < SPLIT:
+                return low_values[:, first:last]
+            return values[:, T + first - SPLIT : T + last - SPLIT]
+
+        def gate(b, first, last):
+            if b == 1:
+                return second_gate[:, first:last]
+            if first < SPLIT:
+                return low_gate[:, first:last]
+            return high_gate[:, DONE + first - SPLIT : DONE + last - SPLIT]
 
         def load_scales(tile, first, last):
             for r in range(SCALE_ROWS):
@@ -76,7 +87,7 @@ def tile_picked_widxput_gate_l_kernel(tc, x_words, x_scales, mem, w1, slot, out)
             nc.sync.dma_start(x_codes[:, first:last].bitcast(I32), x_rows[:, first:last])
 
         def make_gate(b, first, last, bank):
-            scale, start = (early_scale, 0) if first < EARLY else (late_scale, EARLY)
+            scale, start = (late_scale, 0) if first < LATE else (early_scale, LATE)
             acc = psum.tile([P, last - first], F32, name="bank%d" % bank)
             nc.tensor.matmul_mx(
                 out=acc[:],
@@ -87,35 +98,32 @@ def tile_picked_widxput_gate_l_kernel(tc, x_words, x_scales, mem, w1, slot, out)
                 start=True,
                 stop=True,
             )
-            if b == 1 and last == fused_last:
-                nc.scalar.activation(gate[b][:, first:fused_first], acc[:, 0 : fused_first - first], SIGMOID)
-                nc.scalar.activation(fused_gate, acc[:, fused_first - first : last - first], SIGMOID)
+            if b == 1 and last == T:
+                nc.scalar.activation(gate(b, first, T - DONE), acc[:, 0 : T - DONE - first], SIGMOID)
+                nc.scalar.activation(high_gate[:, 0:DONE], acc[:, T - DONE - first : T - first], SIGMOID)
             else:
-                nc.scalar.activation(gate[b][:, first:last], acc[:], SIGMOID)
+                nc.scalar.activation(gate(b, first, last), acc[:], SIGMOID)
 
-        def listed(tile, first, last):
-            return tile[:].indirect(offsets[:, first // LIST_ROWS : last // LIST_ROWS])
+        def listed(b, first, last):
+            return store[b][:].indirect(offsets[:, first // LIST_ROWS : last // LIST_ROWS])
 
         def scalar_gather(b, first, last):
-            nc.scalar.activation(old[b][:, first:last], listed(store[b], first, last), COPY)
+            nc.scalar.activation(old(b, first, last), listed(b, first, last), COPY)
 
         def vector_gather(b, first, last):
-            nc.vector.tensor_copy(old[b][:, first:last], listed(store[b], first, last))
+            nc.vector.tensor_copy(old(b, first, last), listed(b, first, last))
 
-        def products(first, last):
-            multiply(nc.vector, first_new[:, first - FIRST : last - FIRST], 0, first, last)
-
-        def multiply(engine, target, b, first, last):
-            engine.tensor_tensor(target, old[b][:, first:last], gate[b][:, first:last], MULT)
+        def multiply(target, b, first, last):
+            nc.vector.tensor_tensor(target, old(b, first, last), gate(b, first, last), MULT)
 
         nc.sync.dma_start(w_raw[:], w1.rearrange("(p j) c -> p j c", j=PACK))
         nc.scalar.activation(warm_out[:], w_raw[:, 0, 0:WARM_COLUMNS], SIGMOID)
         nc.sync.dma_start(offsets[:], slot)
-        load_scales(early_scale, 0, EARLY)
+        load_scales(early_scale, LATE, T)
         nc.sync.dma_start(store[0][:], mem[0:P, :])
-        load_updates(0, EARLY)
-        load_scales(late_scale, EARLY, T)
-        load_updates(EARLY, T)
+        load_updates(LATE, T)
+        load_scales(late_scale, 0, LATE)
+        load_updates(0, LATE)
         nc.sync.dma_start(store[1][:], mem[P : 2 * P, :])
 
         for b in range(2):
@@ -127,28 +135,28 @@ def tile_picked_widxput_gate_l_kernel(tc, x_words, x_scales, mem, w1, slot, out)
                 in_=w_grouped[b][:].rearrange("p c j -> p (c j)"),
             )
 
-        scalar_gather(0, 0, SCALAR_GATHER[0])
-        vector_gather(0, SCALAR_GATHER[0], T)
-        pieces = [(0, first, first + PIECE) for first in reversed(range(0, EARLY, PIECE))]
-        pieces.extend([(1, 0, 2 * PIECE), (1, 2 * PIECE, EARLY)])
-        for b in range(2):
-            pieces.extend([(b, EARLY, SECOND), (b, SECOND, SECOND + 2 * PIECE), (b, SECOND + 2 * PIECE, T)])
+        scalar_gather(0, T - SCALAR_GATHER[0], T)
+        vector_gather(0, 0, SPLIT)
+        vector_gather(0, SPLIT, T - SCALAR_GATHER[0])
+        pieces = [(0, first, first + PIECE) for first in range(LATE, T, PIECE)]
+        pieces.extend([(1, LATE, T - PIECE), (1, T - PIECE, T)])
+        pieces.extend([(0, SPLIT, LATE), (0, 0, 2 * PIECE), (0, 2 * PIECE, SPLIT)])
+        pieces.extend([(1, 0, 2 * PIECE), (1, 2 * PIECE, 4 * PIECE), (1, 4 * PIECE, LATE)])
         for piece, (b, first, last) in enumerate(pieces):
             make_gate(b, first, last, piece % BANKS)
 
-        products(FIRST, EARLY)
-        multiply(nc.vector, listed(store[0], 0, FIRST), 0, 0, FIRST)
-        products(EARLY, SECOND - HELD)
+        multiply(old(0, LATE, VECTOR_FIRST), 0, LATE, VECTOR_FIRST)
+        multiply(listed(0, VECTOR_FIRST, T), 0, VECTOR_FIRST, T)
 
-        scalar_gather(1, T - SCALAR_GATHER[1], T)
-        nc.vector.tensor_tensor(old[1][:, fused_first:fused_last], listed(store[1], fused_first, fused_last), fused_gate, MULT)
-        vector_gather(1, fused_last, T - SCALAR_GATHER[1])
-        products(SECOND - HELD, SECOND)
-        vector_gather(1, 0, fused_first)
-        multiply(nc.vector, second_new, 0, SECOND, T)
+        scalar_gather(1, T - LEAD, T)
+        scalar_gather(1, T - SCALAR_GATHER[1], T - LEAD)
+        vector_gather(1, 0, T - SCALAR_GATHER[1])
+        both = values[:, T - DONE : T + LATE - SPLIT]
+        nc.gpsimd.tensor_tensor(both, both, high_gate[:, 0 : DONE + LATE - SPLIT], MULT)
+        multiply(second_new, 0, 0, SPLIT)
 
-        nc.scalar.activation(listed(store[0], FIRST, SECOND), first_new, COPY)
-        nc.scalar.activation(listed(store[0], SECOND, T), second_new, COPY)
+        nc.scalar.activation(listed(0, SPLIT, VECTOR_FIRST), old(0, SPLIT, VECTOR_FIRST), COPY)
+        nc.scalar.activation(listed(0, 0, SPLIT), second_new, COPY)
         nc.sync.dma_start(out[0:P, :], store[0][:])
-        multiply(nc.vector, listed(store[1], 0, T), 1, 0, T)
+        multiply(listed(1, 0, T), 1, 0, T)
         nc.sync.dma_start(out[P : 2 * P, :], store[1][:])

@@ -24,9 +24,9 @@ SCALE_ROWS = 4
 BANKS = 8
 PIECE = 128
 LATE = T - 3 * PIECE
-VECTOR_FIRST = 704
+VECTOR_FIRST = 672
 SPLIT = 384
-SCALAR_GATHER = (448, 576)
+SCALAR_GATHER = (448, 640)
 LEAD = 64
 DONE = 8
 WARM_COLUMNS = 8

from contextlib import ExitStack

import concourse.mybir as mybir

K, T, N, U = 512, 1024, 256, 2048
FLOPS = 2 * K * T * N

F32 = mybir.dt.float32
BF16 = mybir.dt.bfloat16
I32 = mybir.dt.int32
U32 = mybir.dt.uint32
U16 = mybir.dt.uint16
U8 = mybir.dt.uint8
FP8X4 = mybir.dt.float8_e4m3fn_x4
SIGMOID = mybir.ActivationFunctionType.Sigmoid
COPY = mybir.ActivationFunctionType.Copy
MULT = mybir.AluOpType.mult

P = 128
PACK = 4
LIST_ROWS = 16
QUADRANT = 32
SCALE_ROWS = 4
BANKS = 8
PIECE = 128
LATE = T - 3 * PIECE
VECTOR_FIRST = 672
SPLIT = 384
SCALAR_GATHER = (448, 640)
LEAD = 64
DONE = 8
WARM_COLUMNS = 8


def tile_picked_widxput_gate_l_kernel(tc, x_words, x_scales, mem, w1, slot, out):
    nc = tc.nc
    with ExitStack() as ctx:
        keep = ctx.enter_context(tc.tile_pool(name="keep", bufs=1))
        psum = ctx.enter_context(tc.psum_pool(name="psum", bufs=1))

        offsets = keep.tile([P, T // LIST_ROWS], U16, name="offsets")
        early_scale = keep.tile([P, T - LATE], U8, name="early_scale", align_bytes=64)
        late_scale = keep.tile([P, LATE], U8, name="late_scale", align_bytes=64)
        x_codes = keep.tile([P, T], U32, name="x_codes", align_bytes=64)
        w_raw = keep.tile([P, PACK, N], F32, name="w_raw", align_bytes=64)
        w_grouped = [keep.tile([P, P, PACK], BF16, name="w_grouped%d" % b, align_bytes=64) for b in range(2)]
        w_codes = [keep.tile([P, P], U32, name="w_codes%d" % b, align_bytes=64) for b in range(2)]
        w_scale = [keep.tile([P, P], U8, name="w_scale%d" % b, align_bytes=64) for b in range(2)]
        store = [keep.tile([P, U], F32, name="store%d" % b, align_bytes=64) for b in range(2)]
        values = keep.tile([P, 2 * T - SPLIT], F32, name="values", align_bytes=64)
        low_values = keep.tile([P, SPLIT], F32, name="low_values", align_bytes=64)
        second_gate = keep.tile([P, T], F32, name="second_gate", align_bytes=64)
        high_gate = keep.tile([P, DONE + T - SPLIT], F32, name="high_gate", align_bytes=64)
        low_gate = keep.tile([P, SPLIT], F32, name="low_gate", align_bytes=64)
        second_new = high_gate[:, DONE : DONE + SPLIT]
        warm_out = keep.tile([P, WARM_COLUMNS], F32, name="warm_out")

        x_rows = x_words[0].rearrange("p c r -> p (c r)").bitcast(I32)
        scale_rows = x_scales[0].bitcast(I32)

        nc.vector.memset(early_scale[:].bitcast(I32), 0)
        nc.vector.memset(late_scale[:].bitcast(I32), 0)
        nc.vector.memset(second_gate[:, T - DONE : T], 1.0)

        def old(b, first, last):
            if b == 1:
                return values[:, first:last]
            if first < SPLIT:
                return low_values[:, first:last]
            return values[:, T + first - SPLIT : T + last - SPLIT]

        def gate(b, first, last):
            if b == 1:
                return second_gate[:, first:last]
            if first < SPLIT:
                return low_gate[:, first:last]
            return high_gate[:, DONE + first - SPLIT : DONE + last - SPLIT]

        def load_scales(tile, first, last):
            for r in range(SCALE_ROWS):
                nc.sync.dma_start(
                    tile[r:P:QUADRANT, :].bitcast(I32),
                    scale_rows[r : P // 8 : SCALE_ROWS, first // PACK : last // PACK],
                )

        def load_updates(first, last):
            nc.sync.dma_start(x_codes[:, first:last].bitcast(I32), x_rows[:, first:last])

        def make_gate(b, first, last, bank):
            scale, start = (late_scale, 0) if first < LATE else (early_scale, LATE)
            acc = psum.tile([P, last - first], F32, name="bank%d" % bank)
            nc.tensor.matmul_mx(
                out=acc[:],
                lhsT=w_codes[b][:].bitcast(FP8X4),
                lhsT_scale=w_scale[b][:],
                rhs=x_codes[:, first:last].bitcast(FP8X4),
                rhs_scale=scale[:, first - start : last - start],
                start=True,
                stop=True,
            )
            if b == 1 and last == T:
                nc.scalar.activation(gate(b, first, T - DONE), acc[:, 0 : T - DONE - first], SIGMOID)
                nc.scalar.activation(high_gate[:, 0:DONE], acc[:, T - DONE - first : T - first], SIGMOID)
            else:
                nc.scalar.activation(gate(b, first, last), acc[:], SIGMOID)

        def listed(b, first, last):
            return store[b][:].indirect(offsets[:, first // LIST_ROWS : last // LIST_ROWS])

        def scalar_gather(b, first, last):
            nc.scalar.activation(old(b, first, last), listed(b, first, last), COPY)

        def vector_gather(b, first, last):
            nc.vector.tensor_copy(old(b, first, last), listed(b, first, last))

        def multiply(target, b, first, last):
            nc.vector.tensor_tensor(target, old(b, first, last), gate(b, first, last), MULT)

        nc.sync.dma_start(w_raw[:], w1.rearrange("(p j) c -> p j c", j=PACK))
        nc.scalar.activation(warm_out[:], w_raw[:, 0, 0:WARM_COLUMNS], SIGMOID)
        nc.sync.dma_start(offsets[:], slot)
        load_scales(early_scale, LATE, T)
        nc.sync.dma_start(store[0][:], mem[0:P, :])
        load_updates(LATE, T)
        load_scales(late_scale, 0, LATE)
        load_updates(0, LATE)
        nc.sync.dma_start(store[1][:], mem[P : 2 * P, :])

        for b in range(2):
            nc.vector.tensor_copy(w_grouped[b][:], w_raw[:, :, b * P : (b + 1) * P].rearrange("p j c -> p c j"))
        for b in range(2):
            nc.vector.quantize_mx(
                out=w_codes[b][:].bitcast(FP8X4),
                scales=w_scale[b][:],
                in_=w_grouped[b][:].rearrange("p c j -> p (c j)"),
            )

        scalar_gather(0, T - SCALAR_GATHER[0], T)
        vector_gather(0, 0, SPLIT)
        vector_gather(0, SPLIT, T - SCALAR_GATHER[0])
        pieces = [(0, first, first + PIECE) for first in range(LATE, T, PIECE)]
        pieces.extend([(1, LATE, T - PIECE), (1, T - PIECE, T)])
        pieces.extend([(0, SPLIT, LATE), (0, 0, 2 * PIECE), (0, 2 * PIECE, SPLIT)])
        pieces.extend([(1, 0, 2 * PIECE), (1, 2 * PIECE, 4 * PIECE), (1, 4 * PIECE, LATE)])
        for piece, (b, first, last) in enumerate(pieces):
            make_gate(b, first, last, piece % BANKS)

        multiply(old(0, LATE, VECTOR_FIRST), 0, LATE, VECTOR_FIRST)
        multiply(listed(0, VECTOR_FIRST, T), 0, VECTOR_FIRST, T)

        scalar_gather(1, T - LEAD, T)
        scalar_gather(1, T - SCALAR_GATHER[1], T - LEAD)
        vector_gather(1, 0, T - SCALAR_GATHER[1])
        both = values[:, T - DONE : T + LATE - SPLIT]
        nc.gpsimd.tensor_tensor(both, both, high_gate[:, 0 : DONE + LATE - SPLIT], MULT)
        multiply(second_new, 0, 0, SPLIT)

        nc.scalar.activation(listed(0, SPLIT, VECTOR_FIRST), old(0, SPLIT, VECTOR_FIRST), COPY)
        nc.scalar.activation(listed(0, 0, SPLIT), second_new, COPY)
        nc.sync.dma_start(out[0:P, :], store[0][:])
        multiply(listed(1, 0, T), 1, 0, T)
        nc.sync.dma_start(out[P : 2 * P, :], store[1][:])
